import numpy as np
import ml_dtypes


def mxq(x, axis, fmt="e4m3"):
    dtype, down = {"e4m3": (ml_dtypes.float8_e4m3fn, 7), "e5m2": (ml_dtypes.float8_e5m2, 14)}[fmt]
    v = np.moveaxis(np.asarray(x, np.float32).astype(ml_dtypes.bfloat16).astype(np.float64), axis, -1)
    blocks = v.reshape(v.shape[:-1] + (-1, 32))
    amax = np.abs(blocks).max(-1, keepdims=True)
    byte = np.maximum(np.where(amax > 0, np.frexp(amax)[1] - 1 + 127, 0) - down, 1)
    scale = np.exp2(byte - 127.0)
    codes = (blocks / scale).astype(np.float32).astype(dtype).astype(np.float64)
    return np.moveaxis((codes * scale).reshape(v.shape), -1, axis)


WIDE = False


def mx_kscale(k):
    if not WIDE:
        return np.ones(k)
    levels = np.array([10, -10, 5, -5, 0])
    if k % 512:
        return np.exp2(np.random.permutation(np.resize(levels, k // 32))).repeat(32)
    a = np.empty((k // 512, 16))
    for p in range(k // 512):
        a[p, :8] = np.random.permutation(np.resize(levels, 8))
        for g in range(8):
            far = levels[np.abs(levels - a[p, g]) >= 10]
            a[p, g + 8] = far[np.random.randint(len(far))]
    return np.exp2(a.ravel()).repeat(32)


def f64(x):
    return np.asarray(x).astype(np.float64)


def striped(idx):
    return np.tile(idx.reshape(-1, 16).T, (8, 1)).astype(np.uint16)


def unstriped(offs):
    return offs[:16].T.reshape(-1).astype(np.int64)


def striped8(idx):
    return np.concatenate([x.reshape(-1, 16).T for x in idx]).astype(np.uint16)


def runs(offs, k):
    lists = np.stack([offs[16 * r : 16 * r + 16].T.reshape(-1) for r in range(8)]).astype(np.int64)
    return lists[np.arange(k) % 512 // 64]


def pack_weight(w):
    k, n = w.shape
    w = f64(np.asarray(w, np.float32).astype(ml_dtypes.bfloat16)).reshape(k // 32, 32, n)
    amax = np.abs(w).max(1)
    byte = np.clip(np.where(amax > 0, np.frexp(amax)[1] - 1 + 127 - 7, 1), 1, 254)
    scaled = (w * np.exp2(127.0 - byte)[:, None, :]).reshape(k, n).astype(np.float32)
    words = np.ascontiguousarray(scaled.reshape(k // 512, 128, 4, n).transpose(0, 1, 3, 2)).astype(ml_dtypes.float8_e4m3fn).view(np.uint8)
    return words, np.ascontiguousarray(byte.astype(np.uint8).reshape(k // 512, 16, n))


def unpack_weight(words, scales):
    g, p, n, _ = words.shape
    vals = np.ascontiguousarray(words).view(ml_dtypes.float8_e4m3fn).astype(np.float64) * np.repeat(np.exp2(scales.astype(np.float64) - 127.0), 8, axis=1)[..., None]
    return vals.transpose(0, 1, 3, 2).reshape(g * 512, n)


K, T, S, N = 512, 2048, 512, 512


def setup_inputs():
    n = np.random.standard_normal
    s = mx_kscale(K)[:, None]
    packed_xT = pack_weight(n((K, T)) * s)
    return {
        "x_words": packed_xT[0],
        "x_scales": packed_xT[1],
        "w1": (n((K, N)) / np.sqrt(K) / s).astype(np.float32),
        "rw": n((N, S)).astype(np.float32),
        "offs": striped(np.random.permutation(T)[:S]),
        "nx": striped8(np.stack([np.random.permutation(S) for _ in range(8)])),
    }


def reference(x_words, x_scales, w1, rw, offs, nx):
    xq = unpack_weight(x_words, x_scales)[:, unstriped(offs)]
    y = mxq(f64(w1), 0, "e4m3").T @ xq
    d = f64(rw) + 0.9 * (y[np.arange(N)[:, None], runs(nx, N)]) - y
    d2 = d + 0.75 * (d[np.arange(N)[:, None], runs(nx, N)])
    return d + 0.75 * (d2[np.arange(N)[:, None], runs(nx, N)])

@@ -1,0 +1,117 @@
+from contextlib import ExitStack
+
+import concourse.mybir as mybir
+
+K, T, S, N = 512, 2048, 512, 512
+FLOPS = 2 * K * N * S
+
+F32 = mybir.dt.float32
+BF16 = mybir.dt.bfloat16
+I32 = mybir.dt.int32
+U32 = mybir.dt.uint32
+U16 = mybir.dt.uint16
+U8 = mybir.dt.uint8
+FP8X4 = mybir.dt.float8_e4m3fn_x4
+ADD = mybir.AluOpType.add
+SUBTRACT = mybir.AluOpType.subtract
+COPY = mybir.ActivationFunctionType.Copy
+
+P = 128
+PACK = 4
+TILES = N // P
+HALF = S // 2
+DISCOUNT = 0.9
+DAMPING = 0.75
+VECTOR_COLUMNS = 84
+
+
+def tile_picked_gae8_none_p_kernel(tc, x_words, x_scales, w1, rw, offs, nx, out):
+    nc = tc.nc
+    rw_rows = rw.rearrange("(p a) j -> a p j", a=TILES)
+    out_rows = out.rearrange("(p a) j -> a p j", a=TILES)
+
+    with ExitStack() as ctx:
+        keep = ctx.enter_context(tc.tile_pool(name="keep", bufs=1))
+        psum = ctx.enter_context(tc.psum_pool(name="psum", bufs=1))
+
+        picks = keep.tile([P, S // 16], U16, name="picks")
+        nexts = keep.tile([P, S // 16], U16, name="nexts")
+        all_words = keep.tile([P, T], U32, name="all_words", align_bytes=64)
+        all_scales = keep.tile([P, T], U8, name="all_scales", align_bytes=64)
+        w_raw = keep.tile([P, PACK, N], F32, name="w_raw")
+        values = [keep.tile([P, 2 * S], F32, name="values%d" % a) for a in range(TILES)]
+        diffs = [keep.tile([P, 2 * S], F32, name="diffs%d" % a) for a in range(TILES)]
+        twos = [keep.tile([P, 2 * S], F32, name="twos%d" % a) for a in range(TILES)]
+        d = [keep.tile([P, S], F32, name="d%d" % a) for a in range(TILES)]
+        result = [keep.tile([P, S], F32, name="result%d" % a) for a in range(TILES)]
+
+        nc.vector.memset(all_scales[:].bitcast(I32), 0)
+        for q in range(4):
+            nc.scalar.dma_start(out=all_scales[32 * q : 32 * q + 4, :].bitcast(I32), in_=x_scales[0, 4 * q : 4 * q + 4, :].bitcast(I32))
+        nc.sync.dma_start(picks[:], offs)
+        nc.sync.dma_start(out=w_raw[:], in_=w1.rearrange("(p t) m -> p t m", t=PACK))
+        nc.sync.dma_start(out=all_words[:].bitcast(I32), in_=x_words[0].rearrange("p c t -> p (c t)").bitcast(I32))
+        nc.sync.dma_start(nexts[:], nx)
+        for a in range(TILES):
+            nc.sync.dma_start(out=values[a][:, S:], in_=rw_rows[a])
+
+        x_scale = keep.tile([P, S], U8, name="x_scale", align_bytes=64)
+        nc.vector.tensor_copy(x_scale[:], all_scales[:].indirect(picks[:]))
+
+        w_bf = keep.tile([P, TILES, P, PACK], BF16, name="w_bf", align_bytes=64)
+        src = w_raw[:].rearrange("p t (c a) -> p c t a", a=TILES)
+        dst = w_bf[:].rearrange("p a c t -> p c t a")
+        nc.vector.tensor_copy(out=dst[:, :VECTOR_COLUMNS], in_=src[:, :VECTOR_COLUMNS])
+        nc.scalar.copy(out=dst[:, VECTOR_COLUMNS:], in_=src[:, VECTOR_COLUMNS:])
+        w_code = keep.tile([P, N], U32, name="w_code", align_bytes=64)
+        w_scale = keep.tile([P, N], U8, name="w_scale", align_bytes=64)
+        nc.vector.quantize_mx(out=w_code[:].bitcast(FP8X4), scales=w_scale[:], in_=w_bf[:].rearrange("p a c t -> p (a c t)"))
+
+        x_code = keep.tile([P, S], U32, name="x_code", align_bytes=64)
+        for h in range(2):
+            nc.vector.tensor_copy(x_code[:, h * HALF : (h + 1) * HALF], all_words[:].indirect(picks[:, h * HALF // 16 : (h + 1) * HALF // 16]))
+
+        def product(a, lo, hi):
+            y = psum.tile([P, hi - lo], F32, name="y%d_%d" % (a, lo))
+            nc.tensor.matmul_mx(
+                out=y[:],
+                lhsT=w_code[:, a * P : (a + 1) * P].bitcast(FP8X4),
+                lhsT_scale=w_scale[:, a * P : (a + 1) * P],
+                rhs=x_code[:, lo:hi].bitcast(FP8X4),
+                rhs_scale=x_scale[:, lo:hi],
+                start=True,
+                stop=True,
+            )
+            return y
+
+        def discounted(a, y, lo, hi):
+            nc.scalar.activation(values[a][:, lo:hi], y[:], COPY, scale=DISCOUNT)
+
+        def reward_less_value(a, y, lo, hi):
+            nc.vector.tensor_tensor(diffs[a][:, S + lo : S + hi], values[a][:, S + lo : S + hi], y[:], SUBTRACT)
+
+        def first_step(a):
+            nc.vector.tensor_tensor(d[a][:], values[a][:].indirect(nexts[:]), diffs[a][:, S:], ADD)
+            nc.scalar.activation(diffs[a][:, :S], d[a][:], COPY, scale=DAMPING * DAMPING)
+            nc.scalar.activation(twos[a][:, S:], d[a][:], COPY, scale=DAMPING)
+
+        for lo in (0, HALF):
+            hi = lo + HALF
+            y0 = product(0, lo, hi)
+            y1 = product(1, lo, hi)
+            reward_less_value(0, y0, lo, hi)
+            discounted(1, y1, lo, hi)
+            reward_less_value(1, y1, lo, hi)
+            discounted(0, y0, lo, hi)
+        for a in (2, 3):
+            y = product(a, 0, S)
+            discounted(a, y, 0, S)
+            first_step(a - 2)
+            reward_less_value(a, y, 0, S)
+        for a in (2, 3):
+            first_step(a)
+        for a in range(TILES):
+            nc.vector.tensor_tensor(twos[a][:, :S], diffs[a][:].indirect(nexts[:]), twos[a][:, S:], ADD)
+        for a in range(TILES):
+            nc.vector.tensor_tensor(result[a][:], twos[a][:].indirect(nexts[:]), d[a][:], ADD)
+            nc.sync.dma_start(out=out_rows[a], in_=result[a][:])

@@ -22,7 +22,6 @@ TILES = N // P
 HALF = S // 2
 DISCOUNT = 0.9
 DAMPING = 0.75
-VECTOR_COLUMNS = 84
 
 
 def tile_picked_gae8_none_p_kernel(tc, x_words, x_scales, w1, rw, offs, nx, out):
@@ -38,7 +37,7 @@ def tile_picked_gae8_none_p_kernel(tc, x_words, x_scales, w1, rw, offs, nx, out)
         nexts = keep.tile([P, S // 16], U16, name="nexts")
         all_words = keep.tile([P, T], U32, name="all_words", align_bytes=64)
         all_scales = keep.tile([P, T], U8, name="all_scales", align_bytes=64)
-        w_raw = keep.tile([P, PACK, N], F32, name="w_raw")
+        w_raw = [keep.tile([P, PACK, N // 2], F32, name="w_raw%d" % h) for h in range(2)]
         values = [keep.tile([P, 2 * S], F32, name="values%d" % a) for a in range(TILES)]
         diffs = [keep.tile([P, 2 * S], F32, name="diffs%d" % a) for a in range(TILES)]
         twos = [keep.tile([P, 2 * S], F32, name="twos%d" % a) for a in range(TILES)]
@@ -46,10 +45,12 @@ def tile_picked_gae8_none_p_kernel(tc, x_words, x_scales, w1, rw, offs, nx, out)
         result = [keep.tile([P, S], F32, name="result%d" % a) for a in range(TILES)]
 
         nc.vector.memset(all_scales[:].bitcast(I32), 0)
-        for q in range(4):
-            nc.scalar.dma_start(out=all_scales[32 * q : 32 * q + 4, :].bitcast(I32), in_=x_scales[0, 4 * q : 4 * q + 4, :].bitcast(I32))
+        w_rows = w1.rearrange("(p t) (h m) -> h p t m", t=PACK, h=2)
+        nc.sync.dma_start(out=w_raw[0][:], in_=w_rows[0])
         nc.sync.dma_start(picks[:], offs)
-        nc.sync.dma_start(out=w_raw[:], in_=w1.rearrange("(p t) m -> p t m", t=PACK))
+        for q in range(4):
+            nc.sync.dma_start(out=all_scales[32 * q : 32 * q + 4, :].bitcast(I32), in_=x_scales[0, 4 * q : 4 * q + 4, :].bitcast(I32))
+        nc.sync.dma_start(out=w_raw[1][:], in_=w_rows[1])
         nc.sync.dma_start(out=all_words[:].bitcast(I32), in_=x_words[0].rearrange("p c t -> p (c t)").bitcast(I32))
         nc.sync.dma_start(nexts[:], nx)
         for a in range(TILES):
@@ -59,10 +60,10 @@ def tile_picked_gae8_none_p_kernel(tc, x_words, x_scales, w1, rw, offs, nx, out)
         nc.vector.tensor_copy(x_scale[:], all_scales[:].indirect(picks[:]))
 
         w_bf = keep.tile([P, TILES, P, PACK], BF16, name="w_bf", align_bytes=64)
-        src = w_raw[:].rearrange("p t (c a) -> p c t a", a=TILES)
+        src = [w_raw[h][:].rearrange("p t (c a) -> p c t a", a=TILES) for h in range(2)]
         dst = w_bf[:].rearrange("p a c t -> p c t a")
-        nc.vector.tensor_copy(out=dst[:, :VECTOR_COLUMNS], in_=src[:, :VECTOR_COLUMNS])
-        nc.scalar.copy(out=dst[:, VECTOR_COLUMNS:], in_=src[:, VECTOR_COLUMNS:])
+        nc.scalar.copy(out=dst[:, : P // 2], in_=src[0])
+        nc.vector.tensor_copy(out=dst[:, P // 2 :], in_=src[1])
         w_code = keep.tile([P, N], U32, name="w_code", align_bytes=64)
         w_scale = keep.tile([P, N], U8, name="w_scale", align_bytes=64)
         nc.vector.quantize_mx(out=w_code[:].bitcast(FP8X4), scales=w_scale[:], in_=w_bf[:].rearrange("p a c t -> p (a c t)"))
@@ -95,14 +96,14 @@ def tile_picked_gae8_none_p_kernel(tc, x_words, x_scales, w1, rw, offs, nx, out)
             nc.scalar.activation(diffs[a][:, :S], d[a][:], COPY, scale=DAMPING * DAMPING)
             nc.scalar.activation(twos[a][:, S:], d[a][:], COPY, scale=DAMPING)
 
-        for lo in (0, HALF):
-            hi = lo + HALF
-            y0 = product(0, lo, hi)
-            y1 = product(1, lo, hi)
-            reward_less_value(0, y0, lo, hi)
-            discounted(1, y1, lo, hi)
-            reward_less_value(1, y1, lo, hi)
-            discounted(0, y0, lo, hi)
+        halves = [(0, HALF), (HALF, S)]
+        ys = {(a, lo): product(a, lo, hi) for lo, hi in halves for a in (0, 1)}
+        for lo, hi in halves:
+            reward_less_value(0, ys[0, lo], lo, hi)
+            discounted(0, ys[0, lo], lo, hi)
+            reward_less_value(1, ys[1, lo], lo, hi)
+        for lo, hi in halves:
+            discounted(1, ys[1, lo], lo, hi)
         for a in (2, 3):
             y = product(a, 0, S)
             discounted(a, y, 0, S)
@@ -113,5 +114,9 @@ def tile_picked_gae8_none_p_kernel(tc, x_words, x_scales, w1, rw, offs, nx, out)
         for a in range(TILES):
             nc.vector.tensor_tensor(twos[a][:, :S], diffs[a][:].indirect(nexts[:]), twos[a][:, S:], ADD)
         for a in range(TILES):
-            nc.vector.tensor_tensor(result[a][:], twos[a][:].indirect(nexts[:]), d[a][:], ADD)
-            nc.sync.dma_start(out=out_rows[a], in_=result[a][:])
+            pieces = 2 if a == TILES - 1 else 1
+            width = S // pieces
+            for lo in range(0, S, width):
+                cols = slice(lo, lo + width)
+                nc.vector.tensor_tensor(result[a][:, cols], twos[a][:].indirect(nexts[:, lo // 16 : (lo + width) // 16]), d[a][:, cols], ADD)
+                nc.sync.dma_start(out=out_rows[a][:, cols], in_=result[a][:, cols])

@@ -1,6 +1,7 @@
 from contextlib import ExitStack
 
 import concourse.mybir as mybir
+from concourse.masks import make_identity
 
 K, T, S, N = 512, 2048, 512, 512
 FLOPS = 2 * K * N * S
@@ -13,15 +14,21 @@ U16 = mybir.dt.uint16
 U8 = mybir.dt.uint8
 FP8X4 = mybir.dt.float8_e4m3fn_x4
 ADD = mybir.AluOpType.add
+MULT = mybir.AluOpType.mult
 SUBTRACT = mybir.AluOpType.subtract
 COPY = mybir.ActivationFunctionType.Copy
 
 P = 128
 PACK = 4
+GROUP = 16
+QUADRANT = 32
+SCALE_ROWS = 4
 TILES = N // P
 HALF = S // 2
 DISCOUNT = 0.9
 DAMPING = 0.75
+ON_VECTOR = (0, 1)
+ON_TENSOR = (2, 3)
 
 
 def tile_picked_gae8_none_p_kernel(tc, x_words, x_scales, w1, rw, offs, nx, out):
@@ -33,23 +40,29 @@ def tile_picked_gae8_none_p_kernel(tc, x_words, x_scales, w1, rw, offs, nx, out)
         keep = ctx.enter_context(tc.tile_pool(name="keep", bufs=1))
         psum = ctx.enter_context(tc.psum_pool(name="psum", bufs=1))
 
-        picks = keep.tile([P, S // 16], U16, name="picks")
-        nexts = keep.tile([P, S // 16], U16, name="nexts")
+        picks = keep.tile([P, S // GROUP], U16, name="picks")
+        nexts = keep.tile([P, S // GROUP], U16, name="nexts")
         all_words = keep.tile([P, T], U32, name="all_words", align_bytes=64)
         all_scales = keep.tile([P, T], U8, name="all_scales", align_bytes=64)
-        w_raw = [keep.tile([P, PACK, N // 2], F32, name="w_raw%d" % h) for h in range(2)]
-        values = [keep.tile([P, 2 * S], F32, name="values%d" % a) for a in range(TILES)]
+        w_raw = [keep.tile([P, PACK // 2, N], F32, name="w_raw%d" % h) for h in range(2)]
+        values = [keep.tile([P, 2 * S], F32, name="values%d" % a, tag="values%d" % a) for a in range(TILES)]
         diffs = [keep.tile([P, 2 * S], F32, name="diffs%d" % a) for a in range(TILES)]
-        twos = [keep.tile([P, 2 * S], F32, name="twos%d" % a) for a in range(TILES)]
-        d = [keep.tile([P, S], F32, name="d%d" % a) for a in range(TILES)]
+        d = {}
         result = [keep.tile([P, S], F32, name="result%d" % a) for a in range(TILES)]
 
+        identity = keep.tile([P, P], F32, name="identity")
+        make_identity(nc, identity[:])
+
         nc.vector.memset(all_scales[:].bitcast(I32), 0)
-        w_rows = w1.rearrange("(p t) (h m) -> h p t m", t=PACK, h=2)
+
+        w_rows = w1.rearrange("(p h t) m -> h p t m", h=2, t=PACK // 2)
         nc.sync.dma_start(out=w_raw[0][:], in_=w_rows[0])
         nc.sync.dma_start(picks[:], offs)
-        for q in range(4):
-            nc.sync.dma_start(out=all_scales[32 * q : 32 * q + 4, :].bitcast(I32), in_=x_scales[0, 4 * q : 4 * q + 4, :].bitcast(I32))
+        for q in range(P // QUADRANT):
+            nc.sync.dma_start(
+                out=all_scales[QUADRANT * q : QUADRANT * q + SCALE_ROWS, :].bitcast(I32),
+                in_=x_scales[0, SCALE_ROWS * q : SCALE_ROWS * (q + 1), :].bitcast(I32),
+            )
         nc.sync.dma_start(out=w_raw[1][:], in_=w_rows[1])
         nc.sync.dma_start(out=all_words[:].bitcast(I32), in_=x_words[0].rearrange("p c t -> p (c t)").bitcast(I32))
         nc.sync.dma_start(nexts[:], nx)
@@ -61,19 +74,20 @@ def tile_picked_gae8_none_p_kernel(tc, x_words, x_scales, w1, rw, offs, nx, out)
 
         w_bf = keep.tile([P, TILES, P, PACK], BF16, name="w_bf", align_bytes=64)
         src = [w_raw[h][:].rearrange("p t (c a) -> p c t a", a=TILES) for h in range(2)]
-        dst = w_bf[:].rearrange("p a c t -> p c t a")
-        nc.scalar.copy(out=dst[:, : P // 2], in_=src[0])
-        nc.vector.tensor_copy(out=dst[:, P // 2 :], in_=src[1])
+        dst = w_bf[:].rearrange("p a c (h t) -> p h c t a", h=2)
+        nc.scalar.copy(out=dst[:, 0], in_=src[0])
+        nc.vector.tensor_copy(out=dst[:, 1], in_=src[1])
         w_code = keep.tile([P, N], U32, name="w_code", align_bytes=64)
         w_scale = keep.tile([P, N], U8, name="w_scale", align_bytes=64)
         nc.vector.quantize_mx(out=w_code[:].bitcast(FP8X4), scales=w_scale[:], in_=w_bf[:].rearrange("p a c t -> p (a c t)"))
 
+        halves = [(0, HALF), (HALF, S)]
         x_code = keep.tile([P, S], U32, name="x_code", align_bytes=64)
-        for h in range(2):
-            nc.vector.tensor_copy(x_code[:, h * HALF : (h + 1) * HALF], all_words[:].indirect(picks[:, h * HALF // 16 : (h + 1) * HALF // 16]))
+        for lo, hi in halves:
+            nc.vector.tensor_copy(x_code[:, lo:hi], all_words[:].indirect(picks[:, lo // GROUP : hi // GROUP]))
 
         def product(a, lo, hi):
-            y = psum.tile([P, hi - lo], F32, name="y%d_%d" % (a, lo))
+            y = psum.tile([P, hi - lo], F32, name="y%d_%d" % (a, lo), tag="bank%d_%d" % (a, lo))
             nc.tensor.matmul_mx(
                 out=y[:],
                 lhsT=w_code[:, a * P : (a + 1) * P].bitcast(FP8X4),
@@ -85,38 +99,80 @@ def tile_picked_gae8_none_p_kernel(tc, x_words, x_scales, w1, rw, offs, nx, out)
             )
             return y
 
-        def discounted(a, y, lo, hi):
-            nc.scalar.activation(values[a][:, lo:hi], y[:], COPY, scale=DISCOUNT)
+        def fill_first_window(a, y, lo, hi, scale):
+            nc.scalar.activation(values[a][:, lo:hi], y[:], COPY, scale=scale)
 
         def reward_less_value(a, y, lo, hi):
             nc.vector.tensor_tensor(diffs[a][:, S + lo : S + hi], values[a][:, S + lo : S + hi], y[:], SUBTRACT)
 
-        def first_step(a):
+        def difference_on_vector(a, tag):
+            d[a] = keep.tile([P, S], F32, name="d%d" % a, tag=tag)
             nc.vector.tensor_tensor(d[a][:], values[a][:].indirect(nexts[:]), diffs[a][:, S:], ADD)
-            nc.scalar.activation(diffs[a][:, :S], d[a][:], COPY, scale=DAMPING * DAMPING)
-            nc.scalar.activation(twos[a][:, S:], d[a][:], COPY, scale=DAMPING)
 
-        halves = [(0, HALF), (HALF, S)]
-        ys = {(a, lo): product(a, lo, hi) for lo, hi in halves for a in (0, 1)}
+        def discounted_next(a):
+            nc.vector.tensor_scalar(diffs[a][:, S:], values[a][:].indirect(nexts[:]), -DISCOUNT, 0.0, MULT, ADD)
+
+        def difference_on_tensor(a):
+            turned = psum.tile([P, S], F32, name="turned%d" % a, tag="turned")
+            terms = (values[a][:, S:], values[a][:, :S], diffs[a][:, S:])
+            for lo in range(0, S, P):
+                for i, term in enumerate(terms):
+                    nc.tensor.matmul(
+                        turned[:, lo : lo + P],
+                        lhsT=term[:, lo : lo + P],
+                        rhs=identity[:],
+                        is_transpose=True,
+                        start=(i == 0),
+                        stop=(i == len(terms) - 1),
+                    )
+            d_turned = keep.tile([P, S], F32, name="d_turned%d" % a, tag="d_turned%d" % a)
+            nc.scalar.copy(d_turned[:], turned[:])
+            back = psum.tile([P, S], F32, name="back%d" % a, tag="bank%d_0" % a)
+            for lo in range(0, S, P):
+                nc.tensor.transpose(back[:, lo : lo + P], d_turned[:, lo : lo + P], identity[:])
+            return back
+
+        def damp_twice(a, source):
+            nc.scalar.activation(diffs[a][:, :S], source[:], COPY, scale=DAMPING * DAMPING)
+
+        def damp_once(a, source):
+            nc.scalar.activation(twos[a][:, S:], source[:], COPY, scale=DAMPING)
+
+        ys = {(a, lo): product(a, lo, hi) for lo, hi in halves for a in ON_VECTOR}
         for lo, hi in halves:
             reward_less_value(0, ys[0, lo], lo, hi)
-            discounted(0, ys[0, lo], lo, hi)
+            fill_first_window(0, ys[0, lo], lo, hi, DISCOUNT)
             reward_less_value(1, ys[1, lo], lo, hi)
         for lo, hi in halves:
-            discounted(1, ys[1, lo], lo, hi)
-        for a in (2, 3):
-            y = product(a, 0, S)
-            discounted(a, y, 0, S)
-            first_step(a - 2)
-            reward_less_value(a, y, 0, S)
-        for a in (2, 3):
-            first_step(a)
+            fill_first_window(1, ys[1, lo], lo, hi, DISCOUNT)
+        for a in ON_TENSOR:
+            fill_first_window(a, product(a, 0, S), 0, S, -1.0)
+
+        difference_on_vector(0, "d0")
+        for a in ON_TENSOR:
+            discounted_next(a)
+        d_in_psum = {2: difference_on_tensor(2)}
+        difference_on_vector(1, "values2")
+
+        twos = [keep.tile([P, 2 * S], F32, name="twos%d" % a) for a in range(TILES)]
+        damp_twice(0, d[0])
+        damp_once(0, d[0])
+        damp_twice(1, d[1])
+        damp_twice(2, d_in_psum[2])
+        damp_once(1, d[1])
+        damp_once(2, d_in_psum[2])
+        d_in_psum[3] = difference_on_tensor(3)
+        damp_twice(3, d_in_psum[3])
+        damp_once(3, d_in_psum[3])
+
         for a in range(TILES):
             nc.vector.tensor_tensor(twos[a][:, :S], diffs[a][:].indirect(nexts[:]), twos[a][:, S:], ADD)
+
         for a in range(TILES):
-            pieces = 2 if a == TILES - 1 else 1
-            width = S // pieces
-            for lo in range(0, S, width):
-                cols = slice(lo, lo + width)
-                nc.vector.tensor_tensor(result[a][:, cols], twos[a][:].indirect(nexts[:, lo // 16 : (lo + width) // 16]), d[a][:, cols], ADD)
-                nc.sync.dma_start(out=out_rows[a][:, cols], in_=result[a][:, cols])
+            if a in ON_TENSOR:
+                d[a] = keep.tile([P, S], F32, name="d%d" % a, tag="d_turned%d" % (sum(ON_TENSOR) - a))
+                nc.scalar.copy(d[a][:], d_in_psum[a][:])
+            for lo, hi in halves if a == TILES - 1 else [(0, S)]:
+                gathered = twos[a][:].indirect(nexts[:, lo // GROUP : hi // GROUP])
+                nc.vector.tensor_tensor(result[a][:, lo:hi], gathered, d[a][:, lo:hi], ADD)
+                nc.sync.dma_start(out=out_rows[a][:, lo:hi], in_=result[a][:, lo:hi])

@@ -27,8 +27,8 @@ TILES = N // P
 HALF = S // 2
 DISCOUNT = 0.9
 DAMPING = 0.75
-ON_VECTOR = (0, 1)
-ON_TENSOR = (2, 3)
+ON_TENSOR = (0, 2, 3)
+ORDER = [1, 0, 2, 3]
 
 
 def tile_picked_gae8_none_p_kernel(tc, x_words, x_scales, w1, rw, offs, nx, out):
@@ -45,9 +45,10 @@ def tile_picked_gae8_none_p_kernel(tc, x_words, x_scales, w1, rw, offs, nx, out)
         all_words = keep.tile([P, T], U32, name="all_words", align_bytes=64)
         all_scales = keep.tile([P, T], U8, name="all_scales", align_bytes=64)
         w_raw = [keep.tile([P, PACK // 2, N], F32, name="w_raw%d" % h) for h in range(2)]
-        values = [keep.tile([P, 2 * S], F32, name="values%d" % a, tag="values%d" % a) for a in range(TILES)]
+        values = [keep.tile([P, 2 * S], F32, name="values%d" % a) for a in range(TILES)]
         diffs = [keep.tile([P, 2 * S], F32, name="diffs%d" % a) for a in range(TILES)]
-        d = {}
+        twos = [keep.tile([P, 2 * S], F32, name="twos%d" % a) for a in range(TILES)]
+        d = [keep.tile([P, S], F32, name="d%d" % a) for a in range(TILES)]
         result = [keep.tile([P, S], F32, name="result%d" % a) for a in range(TILES)]
 
         identity = keep.tile([P, P], F32, name="identity")
@@ -66,7 +67,7 @@ def tile_picked_gae8_none_p_kernel(tc, x_words, x_scales, w1, rw, offs, nx, out)
         nc.sync.dma_start(out=w_raw[1][:], in_=w_rows[1])
         nc.sync.dma_start(out=all_words[:].bitcast(I32), in_=x_words[0].rearrange("p c t -> p (c t)").bitcast(I32))
         nc.sync.dma_start(nexts[:], nx)
-        for a in range(TILES):
+        for a in ORDER:
             nc.sync.dma_start(out=values[a][:, S:], in_=rw_rows[a])
 
         x_scale = keep.tile([P, S], U8, name="x_scale", align_bytes=64)
@@ -105,74 +106,89 @@ def tile_picked_gae8_none_p_kernel(tc, x_words, x_scales, w1, rw, offs, nx, out)
         def reward_less_value(a, y, lo, hi):
             nc.vector.tensor_tensor(diffs[a][:, S + lo : S + hi], values[a][:, S + lo : S + hi], y[:], SUBTRACT)
 
-        def difference_on_vector(a, tag):
-            d[a] = keep.tile([P, S], F32, name="d%d" % a, tag=tag)
-            nc.vector.tensor_tensor(d[a][:], values[a][:].indirect(nexts[:]), diffs[a][:, S:], ADD)
+        turned = {}
 
-        def discounted_next(a):
-            nc.vector.tensor_scalar(diffs[a][:, S:], values[a][:].indirect(nexts[:]), -DISCOUNT, 0.0, MULT, ADD)
-
-        def difference_on_tensor(a):
-            turned = psum.tile([P, S], F32, name="turned%d" % a, tag="turned")
-            terms = (values[a][:, S:], values[a][:, :S], diffs[a][:, S:])
+        def turn(a, term, first, last):
+            if first:
+                turned[a] = psum.tile([P, S], F32, name="turned%d" % a, tag="turned%d" % (ON_TENSOR.index(a) % 2))
             for lo in range(0, S, P):
-                for i, term in enumerate(terms):
-                    nc.tensor.matmul(
-                        turned[:, lo : lo + P],
-                        lhsT=term[:, lo : lo + P],
-                        rhs=identity[:],
-                        is_transpose=True,
-                        start=(i == 0),
-                        stop=(i == len(terms) - 1),
-                    )
-            d_turned = keep.tile([P, S], F32, name="d_turned%d" % a, tag="d_turned%d" % a)
-            nc.scalar.copy(d_turned[:], turned[:])
+                nc.tensor.matmul(
+                    turned[a][:, lo : lo + P],
+                    lhsT=term[:, lo : lo + P],
+                    rhs=identity[:],
+                    is_transpose=True,
+                    start=(first and lo == 0),
+                    stop=(last and lo == S - P),
+                )
+
+        def turn_known(a):
+            turn(a, values[a][:, :S], True, False)
+            turn(a, values[a][:, S:], False, False)
+
+        def turn_back(a):
+            d_turned = keep.tile([P, S], F32, name="d_turned%d" % a, tag="d_turned")
+            nc.scalar.copy(d_turned[:], turned[a][:])
             back = psum.tile([P, S], F32, name="back%d" % a, tag="bank%d_0" % a)
             for lo in range(0, S, P):
                 nc.tensor.transpose(back[:, lo : lo + P], d_turned[:, lo : lo + P], identity[:])
             return back
 
-        def damp_twice(a, source):
+        def damped(a):
+            return twos[ORDER[ORDER.index(a) - 1]][:, S:]
+
+        def damp(a, source):
             nc.scalar.activation(diffs[a][:, :S], source[:], COPY, scale=DAMPING * DAMPING)
+            nc.scalar.activation(damped(a), source[:], COPY, scale=DAMPING)
 
-        def damp_once(a, source):
-            nc.scalar.activation(twos[a][:, S:], source[:], COPY, scale=DAMPING)
+        def second_step(a):
+            nc.vector.tensor_tensor(twos[a][:, :S], diffs[a][:].indirect(nexts[:]), damped(a), ADD)
 
-        ys = {(a, lo): product(a, lo, hi) for lo, hi in halves for a in ON_VECTOR}
-        for lo, hi in halves:
-            reward_less_value(0, ys[0, lo], lo, hi)
-            fill_first_window(0, ys[0, lo], lo, hi, DISCOUNT)
-            reward_less_value(1, ys[1, lo], lo, hi)
-        for lo, hi in halves:
-            fill_first_window(1, ys[1, lo], lo, hi, DISCOUNT)
-        for a in ON_TENSOR:
-            fill_first_window(a, product(a, 0, S), 0, S, -1.0)
-
-        difference_on_vector(0, "d0")
-        for a in ON_TENSOR:
-            discounted_next(a)
-        d_in_psum = {2: difference_on_tensor(2)}
-        difference_on_vector(1, "values2")
-
-        twos = [keep.tile([P, 2 * S], F32, name="twos%d" % a) for a in range(TILES)]
-        damp_twice(0, d[0])
-        damp_once(0, d[0])
-        damp_twice(1, d[1])
-        damp_twice(2, d_in_psum[2])
-        damp_once(1, d[1])
-        damp_once(2, d_in_psum[2])
-        d_in_psum[3] = difference_on_tensor(3)
-        damp_twice(3, d_in_psum[3])
-        damp_once(3, d_in_psum[3])
-
-        for a in range(TILES):
-            nc.vector.tensor_tensor(twos[a][:, :S], diffs[a][:].indirect(nexts[:]), twos[a][:, S:], ADD)
-
-        for a in range(TILES):
-            if a in ON_TENSOR:
-                d[a] = keep.tile([P, S], F32, name="d%d" % a, tag="d_turned%d" % (sum(ON_TENSOR) - a))
-                nc.scalar.copy(d[a][:], d_in_psum[a][:])
+        def third_step(a):
             for lo, hi in halves if a == TILES - 1 else [(0, S)]:
                 gathered = twos[a][:].indirect(nexts[:, lo // GROUP : hi // GROUP])
                 nc.vector.tensor_tensor(result[a][:, lo:hi], gathered, d[a][:, lo:hi], ADD)
                 nc.sync.dma_start(out=out_rows[a][:, lo:hi], in_=result[a][:, lo:hi])
+
+        ys = {(a, lo): product(a, lo, hi) for lo, hi in halves for a in (0, 1)}
+        for a in (2, 3):
+            ys[a, 0] = product(a, 0, S)
+        for lo, hi in halves:
+            fill_first_window(0, ys[0, lo], lo, hi, -1.0)
+            reward_less_value(1, ys[1, lo], lo, hi)
+        for lo, hi in halves:
+            fill_first_window(1, ys[1, lo], lo, hi, DISCOUNT)
+        for a in (2, 3):
+            fill_first_window(a, ys[a, 0], 0, S, -1.0)
+
+        def discounted_next(a):
+            nc.vector.tensor_scalar(diffs[a][:, S:], values[a][:].indirect(nexts[:]), -DISCOUNT, 0.0, MULT, ADD)
+
+        discounted_next(0)
+        nc.vector.tensor_tensor(d[1][:], values[1][:].indirect(nexts[:]), diffs[1][:, S:], ADD)
+        discounted_next(2)
+        discounted_next(3)
+        back = {}
+        turn_known(0)
+        turn(0, diffs[0][:, S:], False, True)
+        turn_known(2)
+        back[0] = turn_back(0)
+        damp(1, d[1])
+        second_step(1)
+        damp(0, back[0])
+        second_step(0)
+        third_step(1)
+        turn(2, diffs[2][:, S:], False, True)
+        turn_known(3)
+        back[2] = turn_back(2)
+        turn(3, diffs[3][:, S:], False, True)
+        damp(2, back[2])
+        nc.scalar.copy(d[0][:], back[0][:])
+        second_step(2)
+        third_step(0)
+        back[3] = turn_back(3)
+        damp(3, back[3])
+        nc.scalar.copy(d[2][:], back[2][:])
+        second_step(3)
+        third_step(2)
+        nc.scalar.copy(d[3][:], back[3][:])
+        third_step(3)

@@ -44,9 +44,10 @@ def tile_picked_gae8_none_p_kernel(tc, x_words, x_scales, w1, rw, offs, nx, out)
         nexts = keep.tile([P, S // GROUP], U16, name="nexts")
         all_words = keep.tile([P, T], U32, name="all_words", align_bytes=64)
         all_scales = keep.tile([P, T], U8, name="all_scales", align_bytes=64)
-        w_raw = [keep.tile([P, PACK // 2, N], F32, name="w_raw%d" % h) for h in range(2)]
+        w_raw = [keep.tile([P, PACK // 2 * N], F32, name="w_raw%d" % h) for h in range(2)]
         values = [keep.tile([P, 2 * S], F32, name="values%d" % a) for a in range(TILES)]
-        diffs = [keep.tile([P, 2 * S], F32, name="diffs%d" % a) for a in range(TILES)]
+        diffs = [w_raw[1]] + [keep.tile([P, 2 * S], F32, name="diffs%d" % a) for a in range(1, TILES)]
+        ahead = {0: diffs[1][:, :S], 2: diffs[2][:, S:], 3: diffs[3][:, S:]}
         twos = [keep.tile([P, 2 * S], F32, name="twos%d" % a) for a in range(TILES)]
         d = [keep.tile([P, S], F32, name="d%d" % a) for a in range(TILES)]
         result = [keep.tile([P, S], F32, name="result%d" % a) for a in range(TILES)]
@@ -56,7 +57,7 @@ def tile_picked_gae8_none_p_kernel(tc, x_words, x_scales, w1, rw, offs, nx, out)
 
         nc.vector.memset(all_scales[:].bitcast(I32), 0)
 
-        w_rows = w1.rearrange("(p h t) m -> h p t m", h=2, t=PACK // 2)
+        w_rows = w1.rearrange("(p h t) m -> h p (t m)", h=2, t=PACK // 2)
         nc.sync.dma_start(out=w_raw[0][:], in_=w_rows[0])
         nc.sync.dma_start(picks[:], offs)
         for q in range(P // QUADRANT):
@@ -74,7 +75,7 @@ def tile_picked_gae8_none_p_kernel(tc, x_words, x_scales, w1, rw, offs, nx, out)
         nc.vector.tensor_copy(x_scale[:], all_scales[:].indirect(picks[:]))
 
         w_bf = keep.tile([P, TILES, P, PACK], BF16, name="w_bf", align_bytes=64)
-        src = [w_raw[h][:].rearrange("p t (c a) -> p c t a", a=TILES) for h in range(2)]
+        src = [w_raw[h][:].rearrange("p (t c a) -> p c t a", t=PACK // 2, a=TILES) for h in range(2)]
         dst = w_bf[:].rearrange("p a c (h t) -> p h c t a", h=2)
         nc.scalar.copy(out=dst[:, 0], in_=src[0])
         nc.vector.tensor_copy(out=dst[:, 1], in_=src[1])
@@ -126,8 +127,8 @@ def tile_picked_gae8_none_p_kernel(tc, x_words, x_scales, w1, rw, offs, nx, out)
             turn(a, values[a][:, S:], False, False)
 
         def turn_back(a):
-            d_turned = keep.tile([P, S], F32, name="d_turned%d" % a, tag="d_turned")
-            nc.scalar.copy(d_turned[:], turned[a][:])
+            d_turned = twos[1][:, :S] if a == 0 else keep.tile([P, S], F32, name="d_turned%d" % a, tag="d_turned")[:]
+            nc.scalar.copy(d_turned, turned[a][:])
             back = psum.tile([P, S], F32, name="back%d" % a, tag="bank%d_0" % a)
             for lo in range(0, S, P):
                 nc.tensor.transpose(back[:, lo : lo + P], d_turned[:, lo : lo + P], identity[:])
@@ -161,7 +162,7 @@ def tile_picked_gae8_none_p_kernel(tc, x_words, x_scales, w1, rw, offs, nx, out)
             fill_first_window(a, ys[a, 0], 0, S, -1.0)
 
         def discounted_next(a):
-            nc.vector.tensor_scalar(diffs[a][:, S:], values[a][:].indirect(nexts[:]), -DISCOUNT, 0.0, MULT, ADD)
+            nc.vector.tensor_scalar(ahead[a], values[a][:].indirect(nexts[:]), -DISCOUNT, 0.0, MULT, ADD)
 
         discounted_next(0)
         nc.vector.tensor_tensor(d[1][:], values[1][:].indirect(nexts[:]), diffs[1][:, S:], ADD)
@@ -169,23 +170,24 @@ def tile_picked_gae8_none_p_kernel(tc, x_words, x_scales, w1, rw, offs, nx, out)
         discounted_next(3)
         back = {}
         turn_known(0)
-        turn(0, diffs[0][:, S:], False, True)
+        turn(0, ahead[0], False, True)
         turn_known(2)
         back[0] = turn_back(0)
-        damp(1, d[1])
-        second_step(1)
+        nc.scalar.activation(diffs[1][:, :S], d[1][:], COPY, scale=DAMPING)
+        nc.vector.tensor_tensor(damped(1), diffs[1][:].indirect(nexts[:]), d[1][:], ADD)
         damp(0, back[0])
         second_step(0)
-        third_step(1)
-        turn(2, diffs[2][:, S:], False, True)
+        turn(2, ahead[2], False, True)
         turn_known(3)
         back[2] = turn_back(2)
-        turn(3, diffs[3][:, S:], False, True)
+        nc.scalar.activation(twos[1][:, :S], damped(1), COPY, scale=DAMPING)
+        third_step(1)
+        turn(3, ahead[3], False, True)
         damp(2, back[2])
+        back[3] = turn_back(3)
         nc.scalar.copy(d[0][:], back[0][:])
         second_step(2)
         third_step(0)
-        back[3] = turn_back(3)
         damp(3, back[3])
         nc.scalar.copy(d[2][:], back[2][:])
         second_step(3)

@@ -60,11 +60,9 @@ def tile_picked_gae8_none_p_kernel(tc, x_words, x_scales, w1, rw, offs, nx, out)
         w_rows = w1.rearrange("(p h t) m -> h p (t m)", h=2, t=PACK // 2)
         nc.sync.dma_start(out=w_raw[0][:], in_=w_rows[0])
         nc.sync.dma_start(picks[:], offs)
-        for q in range(P // QUADRANT):
-            nc.sync.dma_start(
-                out=all_scales[QUADRANT * q : QUADRANT * q + SCALE_ROWS, :].bitcast(I32),
-                in_=x_scales[0, SCALE_ROWS * q : SCALE_ROWS * (q + 1), :].bitcast(I32),
-            )
+        scale_rows = x_scales[0].bitcast(I32).rearrange("(q r) c -> r q c", r=SCALE_ROWS)
+        for r in range(SCALE_ROWS):
+            nc.sync.dma_start(out=all_scales[:].bitcast(I32)[r:P:QUADRANT, :], in_=scale_rows[r])
         nc.sync.dma_start(out=w_raw[1][:], in_=w_rows[1])
         nc.sync.dma_start(out=all_words[:].bitcast(I32), in_=x_words[0].rearrange("p c t -> p (c t)").bitcast(I32))
         nc.sync.dma_start(nexts[:], nx)
@@ -127,7 +125,7 @@ def tile_picked_gae8_none_p_kernel(tc, x_words, x_scales, w1, rw, offs, nx, out)
             turn(a, values[a][:, S:], False, False)
 
         def turn_back(a):
-            d_turned = twos[1][:, :S] if a == 0 else keep.tile([P, S], F32, name="d_turned%d" % a, tag="d_turned")[:]
+            d_turned = twos[1][:, :S] if a == 0 else keep.tile([P, S], F32, name="d_turned%d" % a, tag="d_turned%d" % a)[:]
             nc.scalar.copy(d_turned, turned[a][:])
             back = psum.tile([P, S], F32, name="back%d" % a, tag="bank%d_0" % a)
             for lo in range(0, S, P):
@@ -135,7 +133,7 @@ def tile_picked_gae8_none_p_kernel(tc, x_words, x_scales, w1, rw, offs, nx, out)
             return back
 
         def damped(a):
-            return twos[ORDER[ORDER.index(a) - 1]][:, S:]
+            return twos[{0: 1, 1: 0, 2: 3, 3: 2}[a]][:, S:]
 
         def damp(a, source):
             nc.scalar.activation(diffs[a][:, :S], source[:], COPY, scale=DAMPING * DAMPING)
@@ -151,15 +149,13 @@ def tile_picked_gae8_none_p_kernel(tc, x_words, x_scales, w1, rw, offs, nx, out)
                 nc.sync.dma_start(out=out_rows[a][:, lo:hi], in_=result[a][:, lo:hi])
 
         ys = {(a, lo): product(a, lo, hi) for lo, hi in halves for a in (0, 1)}
-        for a in (2, 3):
-            ys[a, 0] = product(a, 0, S)
+        ys[2, 0] = product(2, 0, S)
         for lo, hi in halves:
             fill_first_window(0, ys[0, lo], lo, hi, -1.0)
             reward_less_value(1, ys[1, lo], lo, hi)
         for lo, hi in halves:
             fill_first_window(1, ys[1, lo], lo, hi, DISCOUNT)
-        for a in (2, 3):
-            fill_first_window(a, ys[a, 0], 0, S, -1.0)
+        fill_first_window(2, ys[2, 0], 0, S, -1.0)
 
         def discounted_next(a):
             nc.vector.tensor_scalar(ahead[a], values[a][:].indirect(nexts[:]), -DISCOUNT, 0.0, MULT, ADD)
@@ -167,30 +163,31 @@ def tile_picked_gae8_none_p_kernel(tc, x_words, x_scales, w1, rw, offs, nx, out)
         discounted_next(0)
         nc.vector.tensor_tensor(d[1][:], values[1][:].indirect(nexts[:]), diffs[1][:, S:], ADD)
         discounted_next(2)
-        discounted_next(3)
         back = {}
         turn_known(0)
         turn(0, ahead[0], False, True)
-        turn_known(2)
+        fill_first_window(3, product(3, 0, S), 0, S, -1.0)
+        discounted_next(3)
         back[0] = turn_back(0)
+        turn_known(2)
         nc.scalar.activation(diffs[1][:, :S], d[1][:], COPY, scale=DAMPING)
         nc.vector.tensor_tensor(damped(1), diffs[1][:].indirect(nexts[:]), d[1][:], ADD)
         damp(0, back[0])
         second_step(0)
         turn(2, ahead[2], False, True)
-        turn_known(3)
         back[2] = turn_back(2)
+        turn_known(3)
+        turn(3, ahead[3], False, True)
         nc.scalar.activation(twos[1][:, :S], damped(1), COPY, scale=DAMPING)
         third_step(1)
-        turn(3, ahead[3], False, True)
-        damp(2, back[2])
-        back[3] = turn_back(3)
         nc.scalar.copy(d[0][:], back[0][:])
-        second_step(2)
         third_step(0)
+        back[3] = turn_back(3)
+        damp(2, back[2])
+        second_step(2)
         damp(3, back[3])
-        nc.scalar.copy(d[2][:], back[2][:])
         second_step(3)
+        nc.scalar.copy(d[2][:], back[2][:])
         third_step(2)
         nc.scalar.copy(d[3][:], back[3][:])
         third_step(3)

@@ -45,10 +45,14 @@ def tile_picked_gae8_none_p_kernel(tc, x_words, x_scales, w1, rw, offs, nx, out)
         all_words = keep.tile([P, T], U32, name="all_words", align_bytes=64)
         all_scales = keep.tile([P, T], U8, name="all_scales", align_bytes=64)
         w_raw = [keep.tile([P, PACK // 2 * N], F32, name="w_raw%d" % h) for h in range(2)]
-        values = [keep.tile([P, 2 * S], F32, name="values%d" % a) for a in range(TILES)]
+        values = {a: keep.tile([P, 2 * S], F32, name="values%d" % a) for a in ON_TENSOR}
+        values[1] = w_raw[0]
+        rewards = {a: values[a][:, S:] for a in ON_TENSOR}
+        rewards[1] = values[2][:, :S]
         diffs = [w_raw[1]] + [keep.tile([P, 2 * S], F32, name="diffs%d" % a) for a in range(1, TILES)]
-        ahead = {0: diffs[1][:, :S], 2: diffs[2][:, S:], 3: diffs[3][:, S:]}
+        ahead = {2: diffs[2][:, S:], 3: diffs[3][:, S:]}
         twos = [keep.tile([P, 2 * S], F32, name="twos%d" % a) for a in range(TILES)]
+        ahead[0] = twos[0][:, S:]
         d = [keep.tile([P, S], F32, name="d%d" % a) for a in range(TILES)]
         result = [keep.tile([P, S], F32, name="result%d" % a) for a in range(TILES)]
 
@@ -67,7 +71,7 @@ def tile_picked_gae8_none_p_kernel(tc, x_words, x_scales, w1, rw, offs, nx, out)
         nc.sync.dma_start(out=all_words[:].bitcast(I32), in_=x_words[0].rearrange("p c t -> p (c t)").bitcast(I32))
         nc.sync.dma_start(nexts[:], nx)
         for a in ORDER:
-            nc.sync.dma_start(out=values[a][:, S:], in_=rw_rows[a])
+            nc.sync.dma_start(out=rewards[a], in_=rw_rows[a])
 
         x_scale = keep.tile([P, S], U8, name="x_scale", align_bytes=64)
         nc.vector.tensor_copy(x_scale[:], all_scales[:].indirect(picks[:]))
@@ -103,7 +107,7 @@ def tile_picked_gae8_none_p_kernel(tc, x_words, x_scales, w1, rw, offs, nx, out)
             nc.scalar.activation(values[a][:, lo:hi], y[:], COPY, scale=scale)
 
         def reward_less_value(a, y, lo, hi):
-            nc.vector.tensor_tensor(diffs[a][:, S + lo : S + hi], values[a][:, S + lo : S + hi], y[:], SUBTRACT)
+            nc.vector.tensor_tensor(diffs[a][:, S + lo : S + hi], rewards[a][:, lo:hi], y[:], SUBTRACT)
 
         turned = {}
 
@@ -125,7 +129,7 @@ def tile_picked_gae8_none_p_kernel(tc, x_words, x_scales, w1, rw, offs, nx, out)
             turn(a, values[a][:, S:], False, False)
 
         def turn_back(a):
-            d_turned = twos[1][:, :S] if a == 0 else keep.tile([P, S], F32, name="d_turned%d" % a, tag="d_turned%d" % a)[:]
+            d_turned = keep.tile([P, S], F32, name="d_turned%d" % a, tag="d_turned%d" % (a == 3))[:]
             nc.scalar.copy(d_turned, turned[a][:])
             back = psum.tile([P, S], F32, name="back%d" % a, tag="bank%d_0" % a)
             for lo in range(0, S, P):
@@ -170,15 +174,15 @@ def tile_picked_gae8_none_p_kernel(tc, x_words, x_scales, w1, rw, offs, nx, out)
         discounted_next(3)
         back[0] = turn_back(0)
         turn_known(2)
-        nc.scalar.activation(diffs[1][:, :S], d[1][:], COPY, scale=DAMPING)
-        nc.vector.tensor_tensor(damped(1), diffs[1][:].indirect(nexts[:]), d[1][:], ADD)
+        nc.scalar.activation(damped(1), d[1][:], COPY, scale=DAMPING)
+        nc.scalar.activation(diffs[1][:, :S], damped(1), COPY, scale=DAMPING)
+        second_step(1)
         damp(0, back[0])
         second_step(0)
         turn(2, ahead[2], False, True)
         back[2] = turn_back(2)
         turn_known(3)
         turn(3, ahead[3], False, True)
-        nc.scalar.activation(twos[1][:, :S], damped(1), COPY, scale=DAMPING)
         third_step(1)
         nc.scalar.copy(d[0][:], back[0][:])
         third_step(0)

@@ -48,13 +48,13 @@ def tile_picked_gae8_none_p_kernel(tc, x_words, x_scales, w1, rw, offs, nx, out)
         values = {a: keep.tile([P, 2 * S], F32, name="values%d" % a) for a in ON_TENSOR}
         values[1] = w_raw[0]
         rewards = {a: values[a][:, S:] for a in ON_TENSOR}
-        rewards[1] = values[2][:, :S]
         diffs = [w_raw[1]] + [keep.tile([P, 2 * S], F32, name="diffs%d" % a) for a in range(1, TILES)]
         ahead = {2: diffs[2][:, S:], 3: diffs[3][:, S:]}
         twos = [keep.tile([P, 2 * S], F32, name="twos%d" % a) for a in range(TILES)]
         ahead[0] = twos[0][:, S:]
         d = [keep.tile([P, S], F32, name="d%d" % a) for a in range(TILES)]
         result = [keep.tile([P, S], F32, name="result%d" % a) for a in range(TILES)]
+        rewards[1] = result[0][:]
 
         identity = keep.tile([P, P], F32, name="identity")
         make_identity(nc, identity[:])
@@ -154,11 +154,13 @@ def tile_picked_gae8_none_p_kernel(tc, x_words, x_scales, w1, rw, offs, nx, out)
 
         ys = {(a, lo): product(a, lo, hi) for lo, hi in halves for a in (0, 1)}
         ys[2, 0] = product(2, 0, S)
-        for lo, hi in halves:
-            fill_first_window(0, ys[0, lo], lo, hi, -1.0)
-            reward_less_value(1, ys[1, lo], lo, hi)
-        for lo, hi in halves:
-            fill_first_window(1, ys[1, lo], lo, hi, DISCOUNT)
+        fill_first_window(0, ys[0, 0], 0, HALF, -1.0)
+        fill_first_window(1, ys[1, 0], 0, HALF, DISCOUNT)
+        reward_less_value(1, ys[1, 0], 0, HALF)
+        fill_first_window(0, ys[0, HALF], HALF, S, -1.0)
+        nc.scalar.activation(result[1][:, HALF:], ys[1, HALF][:], COPY, scale=-1.0)
+        nc.gpsimd.tensor_tensor(diffs[1][:, S + HALF :], rewards[1][:, HALF:], result[1][:, HALF:], ADD)
+        fill_first_window(1, ys[1, HALF], HALF, S, DISCOUNT)
         fill_first_window(2, ys[2, 0], 0, S, -1.0)
 
         def discounted_next(a):

@@ -23,6 +23,7 @@ PACK = 4
 GROUP = 16
 QUADRANT = 32
 SCALE_ROWS = 4
+SPREAD = 8
 TILES = N // P
 HALF = S // 2
 DISCOUNT = 0.9
@@ -42,60 +43,79 @@ def tile_picked_gae8_none_p_kernel(tc, x_words, x_scales, w1, rw, offs, nx, out)
 
         picks = keep.tile([P, S // GROUP], U16, name="picks")
         nexts = keep.tile([P, S // GROUP], U16, name="nexts")
-        all_words = keep.tile([P, T], U32, name="all_words", align_bytes=64)
-        all_scales = keep.tile([P, T], U8, name="all_scales", align_bytes=64)
+        all_words = keep.tile([P, T], U32, name="all_words", tag="words", align_bytes=64)
+        all_scales = keep.tile([P, T], U8, name="all_scales", tag="scales", align_bytes=64)
+        x_scale = keep.tile([P, S], U8, name="x_scale", align_bytes=64)
         w_raw = [keep.tile([P, PACK // 2 * N], F32, name="w_raw%d" % h) for h in range(2)]
-        values = {a: keep.tile([P, 2 * S], F32, name="values%d" % a) for a in ON_TENSOR}
-        values[1] = w_raw[0]
-        rewards = {a: values[a][:, S:] for a in ON_TENSOR}
+        values = {0: w_raw[0], 3: keep.tile([P, 2 * S], F32, name="values3")}
         diffs = [w_raw[1]] + [keep.tile([P, 2 * S], F32, name="diffs%d" % a) for a in range(1, TILES)]
         ahead = {2: diffs[2][:, S:], 3: diffs[3][:, S:]}
         twos = [keep.tile([P, 2 * S], F32, name="twos%d" % a) for a in range(TILES)]
         ahead[0] = twos[0][:, S:]
         d = [keep.tile([P, S], F32, name="d%d" % a) for a in range(TILES)]
         result = [keep.tile([P, S], F32, name="result%d" % a) for a in range(TILES)]
-        rewards[1] = result[0][:]
 
         identity = keep.tile([P, P], F32, name="identity")
         make_identity(nc, identity[:])
 
         nc.vector.memset(all_scales[:].bitcast(I32), 0)
+        nc.vector.memset(x_scale[:].bitcast(I32), 0)
+        nc.vector.memset(values[3][:, S:], 0.0)
 
         w_rows = w1.rearrange("(p h t) m -> h p (t m)", h=2, t=PACK // 2)
         nc.sync.dma_start(out=w_raw[0][:], in_=w_rows[0])
         nc.sync.dma_start(picks[:], offs)
-        scale_rows = x_scales[0].bitcast(I32).rearrange("(q r) c -> r q c", r=SCALE_ROWS)
-        for r in range(SCALE_ROWS):
-            nc.sync.dma_start(out=all_scales[:].bitcast(I32)[r:P:QUADRANT, :], in_=scale_rows[r])
+        nc.sync.dma_start(out=all_scales[:].bitcast(I32)[0:P:SPREAD, :], in_=x_scales[0].bitcast(I32))
         nc.sync.dma_start(out=w_raw[1][:], in_=w_rows[1])
         nc.sync.dma_start(out=all_words[:].bitcast(I32), in_=x_words[0].rearrange("p c t -> p (c t)").bitcast(I32))
         nc.sync.dma_start(nexts[:], nx)
-        for a in ORDER:
-            nc.sync.dma_start(out=rewards[a], in_=rw_rows[a])
 
-        x_scale = keep.tile([P, S], U8, name="x_scale", align_bytes=64)
-        nc.vector.tensor_copy(x_scale[:], all_scales[:].indirect(picks[:]))
+        picked_scales = keep.tile([P, S], U8, name="picked_scales", align_bytes=64)
+        nc.vector.tensor_copy(picked_scales[:], all_scales[:].indirect(picks[:]))
+        for r in range(SCALE_ROWS):
+            nc.sync.dma_start(
+                out=x_scale[:].bitcast(I32)[r:P:QUADRANT, :],
+                in_=picked_scales[:].bitcast(I32)[r * SPREAD : P : QUADRANT, :],
+            )
 
-        w_bf = keep.tile([P, TILES, P, PACK], BF16, name="w_bf", align_bytes=64)
+        w_bf = keep.tile([P, TILES, P, PACK], BF16, name="w_bf", tag="w_bf", align_bytes=64)
         src = [w_raw[h][:].rearrange("p (t c a) -> p c t a", t=PACK // 2, a=TILES) for h in range(2)]
         dst = w_bf[:].rearrange("p a c (h t) -> p h c t a", h=2)
         nc.scalar.copy(out=dst[:, 0], in_=src[0])
-        nc.vector.tensor_copy(out=dst[:, 1], in_=src[1])
-        w_code = keep.tile([P, N], U32, name="w_code", align_bytes=64)
-        w_scale = keep.tile([P, N], U8, name="w_scale", align_bytes=64)
-        nc.vector.quantize_mx(out=w_code[:].bitcast(FP8X4), scales=w_scale[:], in_=w_bf[:].rearrange("p a c t -> p (a c t)"))
+        nc.vector.tensor_copy(out=dst[:, 1, :, :, 0:2], in_=src[1][:, :, :, 0:2])
+        nc.scalar.copy(out=dst[:, 1, :, :, 2:4], in_=src[1][:, :, :, 2:4])
+        w_code, w_scale = {}, {}
 
+        def quantise(pair, tag):
+            w_code[pair] = keep.tile([P, 2 * P], U32, name="w_code%d" % pair, tag=tag, align_bytes=64)
+            w_scale[pair] = keep.tile([P, 2 * P], U8, name="w_scale%d" % pair, align_bytes=64)
+            nc.vector.quantize_mx(
+                out=w_code[pair][:].bitcast(FP8X4),
+                scales=w_scale[pair][:],
+                in_=w_bf[:, 2 * pair : 2 * pair + 2].rearrange("p a c t -> p (a c t)"),
+            )
+
+        quantise(0, "w_code")
+
+        values[1] = keep.tile([P, 2 * S], F32, name="values1", tag="scales", align_bytes=64)
         halves = [(0, HALF), (HALF, S)]
         x_code = keep.tile([P, S], U32, name="x_code", align_bytes=64)
         for lo, hi in halves:
             nc.vector.tensor_copy(x_code[:, lo:hi], all_words[:].indirect(picks[:, lo // GROUP : hi // GROUP]))
+        quantise(1, "words")
+
+        values[2] = keep.tile([P, 2 * S], F32, name="values2", tag="w_bf", align_bytes=64)
+        rewards = {a: values[a][:, S:] for a in range(3)}
+        rewards[3] = diffs[0][:, S:]
+        for a in (1, 0, 3, 2):
+            nc.sync.dma_start(out=rewards[a], in_=rw_rows[a])
 
         def product(a, lo, hi):
             y = psum.tile([P, hi - lo], F32, name="y%d_%d" % (a, lo), tag="bank%d_%d" % (a, lo))
             nc.tensor.matmul_mx(
                 out=y[:],
-                lhsT=w_code[:, a * P : (a + 1) * P].bitcast(FP8X4),
-                lhsT_scale=w_scale[:, a * P : (a + 1) * P],
+                lhsT=w_code[a // 2][:, a % 2 * P : (a % 2 + 1) * P].bitcast(FP8X4),
+                lhsT_scale=w_scale[a // 2][:, a % 2 * P : (a % 2 + 1) * P],
                 rhs=x_code[:, lo:hi].bitcast(FP8X4),
                 rhs_scale=x_scale[:, lo:hi],
                 start=True,
@@ -126,7 +146,7 @@ def tile_picked_gae8_none_p_kernel(tc, x_words, x_scales, w1, rw, offs, nx, out)
 
         def turn_known(a):
             turn(a, values[a][:, :S], True, False)
-            turn(a, values[a][:, S:], False, False)
+            turn(a, rewards[a], False, False)
 
         def turn_back(a):
             d_turned = keep.tile([P, S], F32, name="d_turned%d" % a, tag="d_turned%d" % (a == 3))[:]

@@ -172,11 +172,11 @@ def tile_picked_gae8_none_p_kernel(tc, x_words, x_scales, w1, rw, offs, nx, out)
                 nc.vector.tensor_tensor(result[a][:, lo:hi], gathered, d[a][:, lo:hi], ADD)
                 nc.sync.dma_start(out=out_rows[a][:, lo:hi], in_=result[a][:, lo:hi])
 
-        ys = {(a, lo): product(a, lo, hi) for lo, hi in halves for a in (0, 1)}
+        ys = {(a, lo): product(a, lo, lo + HALF) for a, lo in ((1, 0), (0, 0), (0, HALF), (1, HALF))}
         ys[2, 0] = product(2, 0, S)
-        fill_first_window(0, ys[0, 0], 0, HALF, -1.0)
         fill_first_window(1, ys[1, 0], 0, HALF, DISCOUNT)
         reward_less_value(1, ys[1, 0], 0, HALF)
+        fill_first_window(0, ys[0, 0], 0, HALF, -1.0)
         fill_first_window(0, ys[0, HALF], HALF, S, -1.0)
         nc.scalar.activation(result[1][:, HALF:], ys[1, HALF][:], COPY, scale=-1.0)
         nc.gpsimd.tensor_tensor(diffs[1][:, S + HALF :], rewards[1][:, HALF:], result[1][:, HALF:], ADD)

@@ -1,7 +1,6 @@
 from contextlib import ExitStack
 
 import concourse.mybir as mybir
-from concourse.masks import make_identity
 
 K, T, S, N = 512, 2048, 512, 512
 FLOPS = 2 * K * N * S
@@ -26,10 +25,10 @@ SCALE_ROWS = 4
 SPREAD = 8
 TILES = N // P
 HALF = S // 2
+HALVES = [(0, HALF), (HALF, S)]
 DISCOUNT = 0.9
 DAMPING = 0.75
-ON_TENSOR = (0, 2, 3)
-ORDER = [1, 0, 2, 3]
+RING = 3
 
 
 def tile_picked_gae8_none_p_kernel(tc, x_words, x_scales, w1, rw, offs, nx, out):
@@ -47,20 +46,15 @@ def tile_picked_gae8_none_p_kernel(tc, x_words, x_scales, w1, rw, offs, nx, out)
         all_scales = keep.tile([P, T], U8, name="all_scales", tag="scales", align_bytes=64)
         x_scale = keep.tile([P, S], U8, name="x_scale", align_bytes=64)
         w_raw = [keep.tile([P, PACK // 2 * N], F32, name="w_raw%d" % h) for h in range(2)]
-        values = {0: w_raw[0], 3: keep.tile([P, 2 * S], F32, name="values3")}
-        diffs = [w_raw[1]] + [keep.tile([P, 2 * S], F32, name="diffs%d" % a) for a in range(1, TILES)]
-        ahead = {2: diffs[2][:, S:], 3: diffs[3][:, S:]}
-        twos = [keep.tile([P, 2 * S], F32, name="twos%d" % a) for a in range(TILES)]
-        ahead[0] = twos[0][:, S:]
-        d = [keep.tile([P, S], F32, name="d%d" % a) for a in range(TILES)]
-        result = [keep.tile([P, S], F32, name="result%d" % a) for a in range(TILES)]
 
-        identity = keep.tile([P, P], F32, name="identity")
-        make_identity(nc, identity[:])
+        def row_tiles(name):
+            return [keep.tile([P, S], F32, name="%s%d" % (name, a)) for a in range(TILES)]
+
+        values, less, d, twos, result = (row_tiles(name) for name in ("values", "less", "d", "twos", "result"))
+        ring = [keep.tile([P, S], F32, name="ring%d" % i) for i in range(RING)]
 
         nc.vector.memset(all_scales[:].bitcast(I32), 0)
         nc.vector.memset(x_scale[:].bitcast(I32), 0)
-        nc.vector.memset(values[3][:, S:], 0.0)
 
         w_rows = w1.rearrange("(p h t) m -> h p (t m)", h=2, t=PACK // 2)
         nc.sync.dma_start(out=w_raw[0][:], in_=w_rows[0])
@@ -97,21 +91,22 @@ def tile_picked_gae8_none_p_kernel(tc, x_words, x_scales, w1, rw, offs, nx, out)
 
         quantise(0, "w_code")
 
-        values[1] = keep.tile([P, 2 * S], F32, name="values1", tag="scales", align_bytes=64)
-        halves = [(0, HALF), (HALF, S)]
         x_code = keep.tile([P, S], U32, name="x_code", align_bytes=64)
-        for lo, hi in halves:
+        for lo, hi in HALVES:
             nc.vector.tensor_copy(x_code[:, lo:hi], all_words[:].indirect(picks[:, lo // GROUP : hi // GROUP]))
         quantise(1, "words")
 
-        values[2] = keep.tile([P, 2 * S], F32, name="values2", tag="w_bf", align_bytes=64)
-        rewards = {a: values[a][:, S:] for a in range(3)}
-        rewards[3] = diffs[0][:, S:]
+        rewards = {
+            1: keep.tile([P, S], F32, name="reward1", tag="scales", align_bytes=64)[:],
+            0: w_raw[0][:, S:],
+            3: w_raw[1][:, S:],
+            2: keep.tile([P, S], F32, name="reward2", tag="w_bf", align_bytes=64)[:],
+        }
         for a in (1, 0, 3, 2):
             nc.sync.dma_start(out=rewards[a], in_=rw_rows[a])
 
         def product(a, lo, hi):
-            y = psum.tile([P, hi - lo], F32, name="y%d_%d" % (a, lo), tag="bank%d_%d" % (a, lo))
+            y = psum.tile([P, hi - lo], F32, name="y%d_%d" % (a, lo))
             nc.tensor.matmul_mx(
                 out=y[:],
                 lhsT=w_code[a // 2][:, a % 2 * P : (a % 2 + 1) * P].bitcast(FP8X4),
@@ -123,97 +118,75 @@ def tile_picked_gae8_none_p_kernel(tc, x_words, x_scales, w1, rw, offs, nx, out)
             )
             return y
 
-        def fill_first_window(a, y, lo, hi, scale):
-            nc.scalar.activation(values[a][:, lo:hi], y[:], COPY, scale=scale)
-
-        def reward_less_value(a, y, lo, hi):
-            nc.vector.tensor_tensor(diffs[a][:, S + lo : S + hi], rewards[a][:, lo:hi], y[:], SUBTRACT)
-
-        turned = {}
-
-        def turn(a, term, first, last):
-            if first:
-                turned[a] = psum.tile([P, S], F32, name="turned%d" % a, tag="turned%d" % (ON_TENSOR.index(a) % 2))
-            for lo in range(0, S, P):
-                nc.tensor.matmul(
-                    turned[a][:, lo : lo + P],
-                    lhsT=term[:, lo : lo + P],
-                    rhs=identity[:],
-                    is_transpose=True,
-                    start=(first and lo == 0),
-                    stop=(last and lo == S - P),
-                )
-
-        def turn_known(a):
-            turn(a, values[a][:, :S], True, False)
-            turn(a, rewards[a], False, False)
-
-        def turn_back(a):
-            d_turned = keep.tile([P, S], F32, name="d_turned%d" % a, tag="d_turned%d" % (a == 3))[:]
-            nc.scalar.copy(d_turned, turned[a][:])
-            back = psum.tile([P, S], F32, name="back%d" % a, tag="bank%d_0" % a)
-            for lo in range(0, S, P):
-                nc.tensor.transpose(back[:, lo : lo + P], d_turned[:, lo : lo + P], identity[:])
-            return back
-
-        def damped(a):
-            return twos[{0: 1, 1: 0, 2: 3, 3: 2}[a]][:, S:]
-
-        def damp(a, source):
-            nc.scalar.activation(diffs[a][:, :S], source[:], COPY, scale=DAMPING * DAMPING)
-            nc.scalar.activation(damped(a), source[:], COPY, scale=DAMPING)
-
-        def second_step(a):
-            nc.vector.tensor_tensor(twos[a][:, :S], diffs[a][:].indirect(nexts[:]), damped(a), ADD)
-
-        def third_step(a):
-            for lo, hi in halves if a == TILES - 1 else [(0, S)]:
-                gathered = twos[a][:].indirect(nexts[:, lo // GROUP : hi // GROUP])
-                nc.vector.tensor_tensor(result[a][:, lo:hi], gathered, d[a][:, lo:hi], ADD)
-                nc.sync.dma_start(out=out_rows[a][:, lo:hi], in_=result[a][:, lo:hi])
-
         ys = {(a, lo): product(a, lo, lo + HALF) for a, lo in ((1, 0), (0, 0), (0, HALF), (1, HALF))}
-        ys[2, 0] = product(2, 0, S)
-        fill_first_window(1, ys[1, 0], 0, HALF, DISCOUNT)
-        reward_less_value(1, ys[1, 0], 0, HALF)
-        fill_first_window(0, ys[0, 0], 0, HALF, -1.0)
-        fill_first_window(0, ys[0, HALF], HALF, S, -1.0)
-        nc.scalar.activation(result[1][:, HALF:], ys[1, HALF][:], COPY, scale=-1.0)
-        nc.gpsimd.tensor_tensor(diffs[1][:, S + HALF :], rewards[1][:, HALF:], result[1][:, HALF:], ADD)
-        fill_first_window(1, ys[1, HALF], HALF, S, DISCOUNT)
-        fill_first_window(2, ys[2, 0], 0, S, -1.0)
+        for a in (2, 3):
+            ys[a, 0] = product(a, 0, S)
 
-        def discounted_next(a):
-            nc.vector.tensor_scalar(ahead[a], values[a][:].indirect(nexts[:]), -DISCOUNT, 0.0, MULT, ADD)
+        def fill(a, lo, hi):
+            nc.scalar.activation(values[a][:, lo:hi], ys[a, lo][:], COPY, scale=DISCOUNT if a % 2 else 1.0)
 
-        discounted_next(0)
-        nc.vector.tensor_tensor(d[1][:], values[1][:].indirect(nexts[:]), diffs[1][:, S:], ADD)
-        discounted_next(2)
-        back = {}
-        turn_known(0)
-        turn(0, ahead[0], False, True)
-        fill_first_window(3, product(3, 0, S), 0, S, -1.0)
-        discounted_next(3)
-        back[0] = turn_back(0)
-        turn_known(2)
-        nc.scalar.activation(damped(1), d[1][:], COPY, scale=DAMPING)
-        nc.scalar.activation(diffs[1][:, :S], damped(1), COPY, scale=DAMPING)
-        second_step(1)
-        damp(0, back[0])
-        second_step(0)
-        turn(2, ahead[2], False, True)
-        back[2] = turn_back(2)
-        turn_known(3)
-        turn(3, ahead[3], False, True)
-        third_step(1)
-        nc.scalar.copy(d[0][:], back[0][:])
-        third_step(0)
-        back[3] = turn_back(3)
-        damp(2, back[2])
-        second_step(2)
-        damp(3, back[3])
-        second_step(3)
-        nc.scalar.copy(d[2][:], back[2][:])
-        third_step(2)
-        nc.scalar.copy(d[3][:], back[3][:])
-        third_step(3)
+        def reward_less_value(a, lo, hi):
+            nc.vector.tensor_tensor(less[a][:, lo:hi], rewards[a][:, lo:hi], ys[a, lo][:], SUBTRACT)
+
+        def following(window, lo, hi):
+            return window[:].indirect(nexts[:, lo // GROUP : hi // GROUP])
+
+        fetched = []
+
+        def fetch(window, scale):
+            slot = ring[len(fetched) % RING]
+            fetched.append(slot)
+            for lo, hi in HALVES:
+                nc.scalar.activation(slot[:, lo:hi], following(window, lo, hi), COPY, scale=scale)
+            return slot
+
+        def fetch_add(target, window, plain):
+            for lo, hi in HALVES:
+                nc.vector.tensor_tensor(target[:, lo:hi], following(window, lo, hi), plain[:, lo:hi], ADD)
+
+        def store(a, lo, hi):
+            nc.sync.dma_start(out=out_rows[a][:, lo:hi], in_=result[a][:, lo:hi])
+
+        def add(target, one, other):
+            nc.vector.tensor_tensor(target, one, other, ADD)
+
+        def damp_add(a, got):
+            nc.vector.scalar_tensor_tensor(twos[a][:], d[a][:], DAMPING, got[:], MULT, ADD)
+
+        fill(1, 0, HALF)
+        fill(0, 0, HALF)
+        fill(0, HALF, S)
+        fill(1, HALF, S)
+        reward_less_value(1, 0, HALF)
+        reward_less_value(0, 0, HALF)
+        reward_less_value(0, HALF, S)
+        reward_less_value(1, HALF, S)
+        a1 = fetch(values[0], DISCOUNT)
+        fetch_add(d[1], values[1], less[1])
+        fill(3, 0, S)
+        fill(2, 0, S)
+        add(d[0][:], less[0][:], a1[:])
+        reward_less_value(3, 0, S)
+        c1 = fetch(values[2], DISCOUNT)
+        fetch_add(d[3], values[3], less[3])
+        a2 = fetch(d[0], DAMPING * DAMPING)
+        reward_less_value(2, 0, S)
+        add(d[2][:], less[2][:], c1[:])
+        b2 = fetch(d[1], DAMPING)
+        damp_add(0, a2)
+        c2 = fetch(d[2], DAMPING * DAMPING)
+        fetch_add(result[0], twos[0], d[0])
+        store(0, 0, S)
+        d2 = fetch(d[3], DAMPING)
+        add(twos[1][:], d[1][:], b2[:])
+        damp_add(2, c2)
+        b3 = fetch(twos[1], DAMPING)
+        add(twos[3][:], d[3][:], d2[:])
+        fetch_add(result[2], twos[2], d[2])
+        store(2, 0, S)
+        d3 = fetch(twos[3], DAMPING)
+        add(result[1][:], d[1][:], b3[:])
+        store(1, 0, S)
+        for lo, hi in HALVES:
+            add(result[3][:, lo:hi], d[3][:, lo:hi], d3[:, lo:hi])
+            store(3, lo, hi)

@@ -28,6 +28,7 @@ HALF = S // 2
 HALVES = [(0, HALF), (HALF, S)]
 DISCOUNT = 0.9
 DAMPING = 0.75
+SHARE = 384
 RING = 3
 
 
@@ -50,11 +51,17 @@ def tile_picked_gae8_none_p_kernel(tc, x_words, x_scales, w1, rw, offs, nx, out)
         def row_tiles(name):
             return [keep.tile([P, S], F32, name="%s%d" % (name, a)) for a in range(TILES)]
 
-        values, less, d, twos, result = (row_tiles(name) for name in ("values", "less", "d", "twos", "result"))
+        result = row_tiles("result")
+        values = {a: keep.tile([P, 2 * S], F32, name="values%d" % a) for a in (0, 2)}
+        diffs = {a: keep.tile([P, 2 * S], F32, name="diffs%d" % a) for a in (0, 2)}
+        values[1], diffs[1] = w_raw
+        last = keep.tile([P, S], F32, name="last")
         ring = [keep.tile([P, S], F32, name="ring%d" % i) for i in range(RING)]
 
         nc.vector.memset(all_scales[:].bitcast(I32), 0)
         nc.vector.memset(x_scale[:].bitcast(I32), 0)
+        for a in (0, 2):
+            nc.vector.memset(values[a][:, S:], 0.0)
 
         w_rows = w1.rearrange("(p h t) m -> h p (t m)", h=2, t=PACK // 2)
         nc.sync.dma_start(out=w_raw[0][:], in_=w_rows[0])
@@ -89,19 +96,21 @@ def tile_picked_gae8_none_p_kernel(tc, x_words, x_scales, w1, rw, offs, nx, out)
                 in_=w_bf[:, 2 * pair : 2 * pair + 2].rearrange("p a c t -> p (a c t)"),
             )
 
-        quantise(0, "w_code")
+        quantise(0, "w_code0")
+        quantise(1, "w_code1")
 
         x_code = keep.tile([P, S], U32, name="x_code", align_bytes=64)
         for lo, hi in HALVES:
             nc.vector.tensor_copy(x_code[:, lo:hi], all_words[:].indirect(picks[:, lo // GROUP : hi // GROUP]))
-        quantise(1, "words")
 
-        rewards = {
-            1: keep.tile([P, S], F32, name="reward1", tag="scales", align_bytes=64)[:],
-            0: w_raw[0][:, S:],
-            3: w_raw[1][:, S:],
-            2: keep.tile([P, S], F32, name="reward2", tag="w_bf", align_bytes=64)[:],
-        }
+        values[3] = keep.tile([P, 4 * S], F32, name="values3", tag="scales", align_bytes=64)
+        diffs[3] = keep.tile([P, 2 * S], F32, name="diffs3", tag="w_bf", align_bytes=64)
+        d = {a: diffs[a][:, :S] for a in range(TILES)}
+        rewards = {a: values[3][:, (i + 1) * S : (i + 2) * S] for i, a in enumerate((1, 0, 2))}
+        rewards[3] = diffs[3][:, S:]
+        less = {0: diffs[0][:, S:], 1: rewards[1], 2: diffs[2][:, S:]}
+        twos = {a: values[a][:, :S] for a in range(TILES)}
+        twos[2] = last[:]
         for a in (1, 0, 3, 2):
             nc.sync.dma_start(out=rewards[a], in_=rw_rows[a])
 
@@ -118,8 +127,8 @@ def tile_picked_gae8_none_p_kernel(tc, x_words, x_scales, w1, rw, offs, nx, out)
             )
             return y
 
-        ys = {(a, lo): product(a, lo, lo + HALF) for a, lo in ((1, 0), (0, 0), (0, HALF), (1, HALF))}
-        for a in (2, 3):
+        ys = {(a, lo): product(a, lo, hi) for lo, hi in HALVES for a in (1, 0)}
+        for a in (3, 2):
             ys[a, 0] = product(a, 0, S)
 
         def fill(a, lo, hi):
@@ -133,16 +142,15 @@ def tile_picked_gae8_none_p_kernel(tc, x_words, x_scales, w1, rw, offs, nx, out)
 
         fetched = []
 
-        def fetch(window, scale):
+        def fetch(window, scale, pieces=((0, S),)):
             slot = ring[len(fetched) % RING]
             fetched.append(slot)
-            for lo, hi in HALVES:
+            for lo, hi in pieces:
                 nc.scalar.activation(slot[:, lo:hi], following(window, lo, hi), COPY, scale=scale)
             return slot
 
         def fetch_add(target, window, plain):
-            for lo, hi in HALVES:
-                nc.vector.tensor_tensor(target[:, lo:hi], following(window, lo, hi), plain[:, lo:hi], ADD)
+            nc.vector.tensor_tensor(target, following(window, 0, S), plain, ADD)
 
         def store(a, lo, hi):
             nc.sync.dma_start(out=out_rows[a][:, lo:hi], in_=result[a][:, lo:hi])
@@ -151,42 +159,47 @@ def tile_picked_gae8_none_p_kernel(tc, x_words, x_scales, w1, rw, offs, nx, out)
             nc.vector.tensor_tensor(target, one, other, ADD)
 
         def damp_add(a, got):
-            nc.vector.scalar_tensor_tensor(twos[a][:], d[a][:], DAMPING, got[:], MULT, ADD)
+            nc.vector.scalar_tensor_tensor(twos[a], d[a], DAMPING, got[:], MULT, ADD)
+
+        def less_value(a, lo, hi):
+            nc.vector.tensor_tensor(d[a][:, lo:hi], d[a][:, lo:hi], ys[a, lo][:], SUBTRACT)
 
         fill(1, 0, HALF)
         fill(0, 0, HALF)
-        fill(0, HALF, S)
         fill(1, HALF, S)
+        fill(0, HALF, S)
         reward_less_value(1, 0, HALF)
         reward_less_value(0, 0, HALF)
-        reward_less_value(0, HALF, S)
-        reward_less_value(1, HALF, S)
-        a1 = fetch(values[0], DISCOUNT)
-        fetch_add(d[1], values[1], less[1])
+        fetch_add(d[1], values[1], rewards[1])
         fill(3, 0, S)
+        a1 = fetch(values[0], DISCOUNT)
+        reward_less_value(0, HALF, S)
+        less_value(1, HALF, S)
         fill(2, 0, S)
-        add(d[0][:], less[0][:], a1[:])
-        reward_less_value(3, 0, S)
-        c1 = fetch(values[2], DISCOUNT)
-        fetch_add(d[3], values[3], less[3])
-        a2 = fetch(d[0], DAMPING * DAMPING)
+        fetch_add(d[3], values[3], rewards[3])
+        b2 = fetch(diffs[1], DAMPING * DAMPING)
+        add(d[0], less[0], a1[:])
+        less_value(3, 0, S)
         reward_less_value(2, 0, S)
-        add(d[2][:], less[2][:], c1[:])
-        b2 = fetch(d[1], DAMPING)
-        damp_add(0, a2)
-        c2 = fetch(d[2], DAMPING * DAMPING)
-        fetch_add(result[0], twos[0], d[0])
-        store(0, 0, S)
-        d2 = fetch(d[3], DAMPING)
-        add(twos[1][:], d[1][:], b2[:])
-        damp_add(2, c2)
-        b3 = fetch(twos[1], DAMPING)
-        add(twos[3][:], d[3][:], d2[:])
-        fetch_add(result[2], twos[2], d[2])
-        store(2, 0, S)
-        d3 = fetch(twos[3], DAMPING)
-        add(result[1][:], d[1][:], b3[:])
+        c1 = fetch(values[2], DISCOUNT)
+        damp_add(1, b2)
+        d2 = fetch(diffs[3], DAMPING * DAMPING)
+        add(d[2], less[2], c1[:])
+        fetch_add(result[1][:], values[1], d[1])
         store(1, 0, S)
-        for lo, hi in HALVES:
-            add(result[3][:, lo:hi], d[3][:, lo:hi], d3[:, lo:hi])
-            store(3, lo, hi)
+        a2 = fetch(diffs[0], DAMPING)
+        damp_add(3, d2)
+        c2 = fetch(diffs[2], DAMPING * DAMPING)
+        add(twos[0], d[0], a2[:])
+        fetch_add(result[3][:], values[3], d[3])
+        store(3, 0, S)
+        a3 = fetch(values[0], DAMPING)
+        damp_add(2, c2)
+        c3 = fetch(last, 1.0, [(0, HALF), (HALF, SHARE)])
+        add(result[0][:], d[0], a3[:])
+        store(0, 0, S)
+        nc.vector.tensor_tensor(result[2][:, SHARE:], following(last, SHARE, S), d[2][:, SHARE:], ADD)
+        add(result[2][:, :HALF], d[2][:, :HALF], c3[:, :HALF])
+        store(2, 0, HALF)
+        add(result[2][:, HALF:SHARE], d[2][:, HALF:SHARE], c3[:, HALF:SHARE])
+        store(2, HALF, S)

@@ -28,7 +28,6 @@ HALF = S // 2
 HALVES = [(0, HALF), (HALF, S)]
 DISCOUNT = 0.9
 DAMPING = 0.75
-SHARE = 384
 RING = 3
 
 
@@ -52,16 +51,14 @@ def tile_picked_gae8_none_p_kernel(tc, x_words, x_scales, w1, rw, offs, nx, out)
             return [keep.tile([P, S], F32, name="%s%d" % (name, a)) for a in range(TILES)]
 
         result = row_tiles("result")
-        values = {a: keep.tile([P, 2 * S], F32, name="values%d" % a) for a in (0, 2)}
+        values = {0: keep.tile([P, 2 * S], F32, name="values0")}
         diffs = {a: keep.tile([P, 2 * S], F32, name="diffs%d" % a) for a in (0, 2)}
         values[1], diffs[1] = w_raw
-        last = keep.tile([P, S], F32, name="last")
         ring = [keep.tile([P, S], F32, name="ring%d" % i) for i in range(RING)]
 
         nc.vector.memset(all_scales[:].bitcast(I32), 0)
         nc.vector.memset(x_scale[:].bitcast(I32), 0)
-        for a in (0, 2):
-            nc.vector.memset(values[a][:, S:], 0.0)
+        nc.vector.memset(values[0][:, S:], 0.0)
 
         w_rows = w1.rearrange("(p h t) m -> h p (t m)", h=2, t=PACK // 2)
         nc.sync.dma_start(out=w_raw[0][:], in_=w_rows[0])
@@ -71,7 +68,7 @@ def tile_picked_gae8_none_p_kernel(tc, x_words, x_scales, w1, rw, offs, nx, out)
         nc.sync.dma_start(out=all_words[:].bitcast(I32), in_=x_words[0].rearrange("p c t -> p (c t)").bitcast(I32))
         nc.sync.dma_start(nexts[:], nx)
 
-        picked_scales = keep.tile([P, S], U8, name="picked_scales", align_bytes=64)
+        picked_scales = keep.tile([P, S], U8, name="picked_scales", tag="picked", align_bytes=64)
         nc.vector.tensor_copy(picked_scales[:], all_scales[:].indirect(picks[:]))
         for r in range(SCALE_ROWS):
             nc.sync.dma_start(
@@ -103,14 +100,13 @@ def tile_picked_gae8_none_p_kernel(tc, x_words, x_scales, w1, rw, offs, nx, out)
         for lo, hi in HALVES:
             nc.vector.tensor_copy(x_code[:, lo:hi], all_words[:].indirect(picks[:, lo // GROUP : hi // GROUP]))
 
-        values[3] = keep.tile([P, 4 * S], F32, name="values3", tag="scales", align_bytes=64)
+        values[3] = keep.tile([P, 2 * S], F32, name="values3", tag="scales", align_bytes=64)
+        values[2] = keep.tile([P, 2 * S], F32, name="values2", tag="picked", align_bytes=64)
         diffs[3] = keep.tile([P, 2 * S], F32, name="diffs3", tag="w_bf", align_bytes=64)
         d = {a: diffs[a][:, :S] for a in range(TILES)}
-        rewards = {a: values[3][:, (i + 1) * S : (i + 2) * S] for i, a in enumerate((1, 0, 2))}
-        rewards[3] = diffs[3][:, S:]
+        rewards = {0: diffs[1][:, S:], 1: values[3][:, S:], 2: values[2][:, S:], 3: diffs[3][:, S:]}
         less = {0: diffs[0][:, S:], 1: rewards[1], 2: diffs[2][:, S:]}
         twos = {a: values[a][:, :S] for a in range(TILES)}
-        twos[2] = last[:]
         for a in (1, 0, 3, 2):
             nc.sync.dma_start(out=rewards[a], in_=rw_rows[a])
 
@@ -127,7 +123,7 @@ def tile_picked_gae8_none_p_kernel(tc, x_words, x_scales, w1, rw, offs, nx, out)
             )
             return y
 
-        ys = {(a, lo): product(a, lo, hi) for lo, hi in HALVES for a in (1, 0)}
+        ys = {(a, lo): product(a, lo, hi) for a, (lo, hi) in zip((1, 0, 0, 1), (HALVES[0], HALVES[0], HALVES[1], HALVES[1]))}
         for a in (3, 2):
             ys[a, 0] = product(a, 0, S)
 
@@ -149,8 +145,8 @@ def tile_picked_gae8_none_p_kernel(tc, x_words, x_scales, w1, rw, offs, nx, out)
                 nc.scalar.activation(slot[:, lo:hi], following(window, lo, hi), COPY, scale=scale)
             return slot
 
-        def fetch_add(target, window, plain):
-            nc.vector.tensor_tensor(target, following(window, 0, S), plain, ADD)
+        def fetch_add(target, window, plain, lo=0, hi=S):
+            nc.vector.tensor_tensor(target[:, lo:hi], following(window, lo, hi), plain[:, lo:hi], ADD)
 
         def store(a, lo, hi):
             nc.sync.dma_start(out=out_rows[a][:, lo:hi], in_=result[a][:, lo:hi])
@@ -166,40 +162,38 @@ def tile_picked_gae8_none_p_kernel(tc, x_words, x_scales, w1, rw, offs, nx, out)
 
         fill(1, 0, HALF)
         fill(0, 0, HALF)
-        fill(1, HALF, S)
         fill(0, HALF, S)
+        fill(1, HALF, S)
         reward_less_value(1, 0, HALF)
         reward_less_value(0, 0, HALF)
+        reward_less_value(0, HALF, S)
+        a1 = fetch(values[0], DISCOUNT)
         fetch_add(d[1], values[1], rewards[1])
         fill(3, 0, S)
-        a1 = fetch(values[0], DISCOUNT)
-        reward_less_value(0, HALF, S)
-        less_value(1, HALF, S)
+        add(d[0], less[0], a1[:])
         fill(2, 0, S)
+        less_value(1, HALF, S)
+        a2 = fetch(diffs[0], DAMPING)
         fetch_add(d[3], values[3], rewards[3])
         b2 = fetch(diffs[1], DAMPING * DAMPING)
-        add(d[0], less[0], a1[:])
-        less_value(3, 0, S)
         reward_less_value(2, 0, S)
+        less_value(3, 0, S)
         c1 = fetch(values[2], DISCOUNT)
+        add(twos[0], d[0], a2[:])
         damp_add(1, b2)
         d2 = fetch(diffs[3], DAMPING * DAMPING)
         add(d[2], less[2], c1[:])
         fetch_add(result[1][:], values[1], d[1])
         store(1, 0, S)
-        a2 = fetch(diffs[0], DAMPING)
+        c2 = fetch(diffs[2], DAMPING)
         damp_add(3, d2)
-        c2 = fetch(diffs[2], DAMPING * DAMPING)
-        add(twos[0], d[0], a2[:])
-        fetch_add(result[3][:], values[3], d[3])
-        store(3, 0, S)
         a3 = fetch(values[0], DAMPING)
-        damp_add(2, c2)
-        c3 = fetch(last, 1.0, [(0, HALF), (HALF, SHARE)])
-        add(result[0][:], d[0], a3[:])
-        store(0, 0, S)
-        nc.vector.tensor_tensor(result[2][:, SHARE:], following(last, SHARE, S), d[2][:, SHARE:], ADD)
-        add(result[2][:, :HALF], d[2][:, :HALF], c3[:, :HALF])
-        store(2, 0, HALF)
-        add(result[2][:, HALF:SHARE], d[2][:, HALF:SHARE], c3[:, HALF:SHARE])
-        store(2, HALF, S)
+        add(twos[2], d[2], c2[:])
+        for lo, hi in HALVES:
+            fetch_add(result[3][:], values[3], d[3], lo, hi)
+            store(3, lo, hi)
+        c3 = fetch(values[2], DAMPING, HALVES)
+        for a, got in ((0, a3), (2, c3)):
+            for lo, hi in HALVES:
+                add(result[a][:, lo:hi], d[a][:, lo:hi], got[:, lo:hi])
+                store(a, lo, hi)

@@ -51,14 +51,15 @@ def tile_picked_gae8_none_p_kernel(tc, x_words, x_scales, w1, rw, offs, nx, out)
             return [keep.tile([P, S], F32, name="%s%d" % (name, a)) for a in range(TILES)]
 
         result = row_tiles("result")
-        values = {0: keep.tile([P, 2 * S], F32, name="values0")}
-        diffs = {a: keep.tile([P, 2 * S], F32, name="diffs%d" % a) for a in (0, 2)}
+        values = {a: keep.tile([P, 2 * S], F32, name="values%d" % a) for a in (0, 2)}
+        diffs = {a: keep.tile([P, 2 * S], F32, name="diffs%d" % a) for a in (2, 3)}
         values[1], diffs[1] = w_raw
         ring = [keep.tile([P, S], F32, name="ring%d" % i) for i in range(RING)]
 
         nc.vector.memset(all_scales[:].bitcast(I32), 0)
         nc.vector.memset(x_scale[:].bitcast(I32), 0)
-        nc.vector.memset(values[0][:, S:], 0.0)
+        for spare in (values[0], values[2], diffs[3]):
+            nc.vector.memset(spare[:, S:], 0.0)
 
         w_rows = w1.rearrange("(p h t) m -> h p (t m)", h=2, t=PACK // 2)
         nc.sync.dma_start(out=w_raw[0][:], in_=w_rows[0])
@@ -101,11 +102,10 @@ def tile_picked_gae8_none_p_kernel(tc, x_words, x_scales, w1, rw, offs, nx, out)
             nc.vector.tensor_copy(x_code[:, lo:hi], all_words[:].indirect(picks[:, lo // GROUP : hi // GROUP]))
 
         values[3] = keep.tile([P, 2 * S], F32, name="values3", tag="scales", align_bytes=64)
-        values[2] = keep.tile([P, 2 * S], F32, name="values2", tag="picked", align_bytes=64)
-        diffs[3] = keep.tile([P, 2 * S], F32, name="diffs3", tag="w_bf", align_bytes=64)
+        diffs[0] = keep.tile([P, 2 * S], F32, name="diffs0", tag="w_bf", align_bytes=64)
         d = {a: diffs[a][:, :S] for a in range(TILES)}
-        rewards = {0: diffs[1][:, S:], 1: values[3][:, S:], 2: values[2][:, S:], 3: diffs[3][:, S:]}
-        less = {0: diffs[0][:, S:], 1: rewards[1], 2: diffs[2][:, S:]}
+        rewards = {0: diffs[1][:, S:], 1: values[3][:, S:], 2: diffs[0][:, S:], 3: diffs[0][:, :S]}
+        less = {0: rewards[0], 1: rewards[1], 2: diffs[2][:, S:]}
         twos = {a: values[a][:, :S] for a in range(TILES)}
         for a in (1, 0, 3, 2):
             nc.sync.dma_start(out=rewards[a], in_=rw_rows[a])
@@ -166,34 +166,37 @@ def tile_picked_gae8_none_p_kernel(tc, x_words, x_scales, w1, rw, offs, nx, out)
         fill(1, HALF, S)
         reward_less_value(1, 0, HALF)
         reward_less_value(0, 0, HALF)
-        reward_less_value(0, HALF, S)
-        a1 = fetch(values[0], DISCOUNT)
+        a1 = result[0]
+        nc.scalar.activation(a1[:], following(values[0], 0, S), COPY, scale=DISCOUNT)
         fetch_add(d[1], values[1], rewards[1])
         fill(3, 0, S)
-        add(d[0], less[0], a1[:])
+        reward_less_value(0, HALF, S)
         fill(2, 0, S)
         less_value(1, HALF, S)
-        a2 = fetch(diffs[0], DAMPING)
-        fetch_add(d[3], values[3], rewards[3])
         b2 = fetch(diffs[1], DAMPING * DAMPING)
+        fetch_add(d[3], values[3], rewards[3])
+        nc.gpsimd.tensor_tensor(d[0], less[0], a1[:], ADD)
+        c1 = fetch(values[2], DISCOUNT)
         reward_less_value(2, 0, S)
         less_value(3, 0, S)
-        c1 = fetch(values[2], DISCOUNT)
-        add(twos[0], d[0], a2[:])
-        damp_add(1, b2)
         d2 = fetch(diffs[3], DAMPING * DAMPING)
+        damp_add(1, b2)
         add(d[2], less[2], c1[:])
+        a2 = fetch(diffs[0], DAMPING)
         fetch_add(result[1][:], values[1], d[1])
         store(1, 0, S)
         c2 = fetch(diffs[2], DAMPING)
         damp_add(3, d2)
+        add(twos[0], d[0], a2[:])
         a3 = fetch(values[0], DAMPING)
+        fetch_add(result[3][:], values[3], d[3], 0, HALF)
+        store(3, 0, HALF)
         add(twos[2], d[2], c2[:])
-        for lo, hi in HALVES:
-            fetch_add(result[3][:], values[3], d[3], lo, hi)
-            store(3, lo, hi)
+        fetch_add(result[3][:], values[3], d[3], HALF, S)
+        store(3, HALF, S)
         c3 = fetch(values[2], DAMPING, HALVES)
-        for a, got in ((0, a3), (2, c3)):
-            for lo, hi in HALVES:
-                add(result[a][:, lo:hi], d[a][:, lo:hi], got[:, lo:hi])
-                store(a, lo, hi)
+        add(result[0][:], d[0], a3[:])
+        store(0, 0, S)
+        for lo, hi in HALVES:
+            add(result[2][:, lo:hi], d[2][:, lo:hi], c3[:, lo:hi])
+            store(2, lo, hi)

@@ -28,6 +28,7 @@ HALF = S // 2
 HALVES = [(0, HALF), (HALF, S)]
 DISCOUNT = 0.9
 DAMPING = 0.75
+SHARE = 384
 RING = 3
 
 
@@ -106,7 +107,9 @@ def tile_picked_gae8_none_p_kernel(tc, x_words, x_scales, w1, rw, offs, nx, out)
         d = {a: diffs[a][:, :S] for a in range(TILES)}
         rewards = {0: diffs[1][:, S:], 1: values[3][:, S:], 2: diffs[0][:, S:], 3: diffs[0][:, :S]}
         less = {0: rewards[0], 1: rewards[1], 2: diffs[2][:, S:]}
+        last = keep.tile([P, S], F32, name="last")
         twos = {a: values[a][:, :S] for a in range(TILES)}
+        twos[2] = last[:]
         for a in (1, 0, 3, 2):
             nc.sync.dma_start(out=rewards[a], in_=rw_rows[a])
 
@@ -185,18 +188,20 @@ def tile_picked_gae8_none_p_kernel(tc, x_words, x_scales, w1, rw, offs, nx, out)
         a2 = fetch(diffs[0], DAMPING)
         fetch_add(result[1][:], values[1], d[1])
         store(1, 0, S)
-        c2 = fetch(diffs[2], DAMPING)
+        c2 = fetch(diffs[2], DAMPING * DAMPING)
         damp_add(3, d2)
         add(twos[0], d[0], a2[:])
         a3 = fetch(values[0], DAMPING)
         fetch_add(result[3][:], values[3], d[3], 0, HALF)
         store(3, 0, HALF)
-        add(twos[2], d[2], c2[:])
+        damp_add(2, c2)
         fetch_add(result[3][:], values[3], d[3], HALF, S)
         store(3, HALF, S)
-        c3 = fetch(values[2], DAMPING, HALVES)
+        c3 = fetch(last, 1.0, [(0, HALF), (HALF, SHARE)])
         add(result[0][:], d[0], a3[:])
         store(0, 0, S)
-        for lo, hi in HALVES:
-            add(result[2][:, lo:hi], d[2][:, lo:hi], c3[:, lo:hi])
-            store(2, lo, hi)
+        add(result[2][:, :HALF], d[2][:, :HALF], c3[:, :HALF])
+        store(2, 0, HALF)
+        fetch_add(result[2][:], last, d[2], SHARE, S)
+        add(result[2][:, HALF:SHARE], d[2][:, HALF:SHARE], c3[:, HALF:SHARE])
+        store(2, HALF, S)

@@ -103,14 +103,14 @@ def tile_picked_gae8_none_p_kernel(tc, x_words, x_scales, w1, rw, offs, nx, out)
             nc.vector.tensor_copy(x_code[:, lo:hi], all_words[:].indirect(picks[:, lo // GROUP : hi // GROUP]))
 
         values[3] = keep.tile([P, 2 * S], F32, name="values3", tag="scales", align_bytes=64)
-        diffs[0] = keep.tile([P, 2 * S], F32, name="diffs0", tag="w_bf", align_bytes=64)
+        diffs[0] = keep.tile([P, HALF + 2 * S], F32, name="diffs0", tag="w_bf", align_bytes=64)
         d = {a: diffs[a][:, :S] for a in range(TILES)}
-        rewards = {0: diffs[1][:, S:], 1: values[3][:, S:], 2: diffs[0][:, S:], 3: diffs[0][:, :S]}
+        rewards = {0: diffs[1][:, S:], 1: values[3][:, S:], 2: diffs[0][:, HALF + S :], 3: diffs[0][:, HALF : HALF + S]}
         less = {0: rewards[0], 1: rewards[1], 2: diffs[2][:, S:]}
         last = keep.tile([P, S], F32, name="last")
         twos = {a: values[a][:, :S] for a in range(TILES)}
         twos[2] = last[:]
-        for a in (1, 0, 3, 2):
+        for a in (1, 0, 2, 3):
             nc.sync.dma_start(out=rewards[a], in_=rw_rows[a])
 
         def product(a, lo, hi):
@@ -127,8 +127,9 @@ def tile_picked_gae8_none_p_kernel(tc, x_words, x_scales, w1, rw, offs, nx, out)
             return y
 
         ys = {(a, lo): product(a, lo, hi) for a, (lo, hi) in zip((1, 0, 0, 1), (HALVES[0], HALVES[0], HALVES[1], HALVES[1]))}
-        for a in (3, 2):
-            ys[a, 0] = product(a, 0, S)
+        ys[2, 0] = product(2, 0, HALF)
+        ys[3, 0] = product(3, 0, S)
+        ys[2, HALF] = product(2, HALF, S)
 
         def fill(a, lo, hi):
             nc.scalar.activation(values[a][:, lo:hi], ys[a, lo][:], COPY, scale=DISCOUNT if a % 2 else 1.0)
@@ -168,19 +169,23 @@ def tile_picked_gae8_none_p_kernel(tc, x_words, x_scales, w1, rw, offs, nx, out)
         fill(0, HALF, S)
         fill(1, HALF, S)
         reward_less_value(1, 0, HALF)
-        reward_less_value(0, 0, HALF)
+        early = keep.tile([P, HALF], F32, name="early")
+        nc.gpsimd.tensor_tensor(early[:], rewards[0][:, :HALF], values[0][:, :HALF], SUBTRACT)
+        reward_less_value(0, HALF, S)
         a1 = result[0]
         nc.scalar.activation(a1[:], following(values[0], 0, S), COPY, scale=DISCOUNT)
         fetch_add(d[1], values[1], rewards[1])
         fill(3, 0, S)
-        reward_less_value(0, HALF, S)
-        fill(2, 0, S)
+        reward_less_value(2, 0, HALF)
+        nc.gpsimd.tensor_tensor(d[0][:, :HALF], early[:], a1[:, :HALF], ADD)
+        fill(2, HALF, S)
+        fill(2, 0, HALF)
         less_value(1, HALF, S)
         b2 = fetch(diffs[1], DAMPING * DAMPING)
         fetch_add(d[3], values[3], rewards[3])
-        nc.gpsimd.tensor_tensor(d[0], less[0], a1[:], ADD)
+        nc.gpsimd.tensor_tensor(d[0][:, HALF:], less[0][:, HALF:], a1[:, HALF:], ADD)
         c1 = fetch(values[2], DISCOUNT)
-        reward_less_value(2, 0, S)
+        reward_less_value(2, HALF, S)
         less_value(3, 0, S)
         d2 = fetch(diffs[3], DAMPING * DAMPING)
         damp_add(1, b2)

@@ -52,14 +52,14 @@ def tile_picked_gae8_none_p_kernel(tc, x_words, x_scales, w1, rw, offs, nx, out)
             return [keep.tile([P, S], F32, name="%s%d" % (name, a)) for a in range(TILES)]
 
         result = row_tiles("result")
-        values = {a: keep.tile([P, 2 * S], F32, name="values%d" % a) for a in (0, 2)}
+        values = {0: keep.tile([P, 2 * S], F32, name="values0"), 2: keep.tile([P, S], F32, name="values2")}
         diffs = {a: keep.tile([P, 2 * S], F32, name="diffs%d" % a) for a in (2, 3)}
         values[1], diffs[1] = w_raw
         ring = [keep.tile([P, S], F32, name="ring%d" % i) for i in range(RING)]
 
         nc.vector.memset(all_scales[:].bitcast(I32), 0)
         nc.vector.memset(x_scale[:].bitcast(I32), 0)
-        for spare in (values[0], values[2], diffs[3]):
+        for spare in (values[0], diffs[3]):
             nc.vector.memset(spare[:, S:], 0.0)
 
         w_rows = w1.rearrange("(p h t) m -> h p (t m)", h=2, t=PACK // 2)
@@ -107,9 +107,7 @@ def tile_picked_gae8_none_p_kernel(tc, x_words, x_scales, w1, rw, offs, nx, out)
         d = {a: diffs[a][:, :S] for a in range(TILES)}
         rewards = {0: diffs[1][:, S:], 1: values[3][:, S:], 2: diffs[0][:, HALF + S :], 3: diffs[0][:, HALF : HALF + S]}
         less = {0: rewards[0], 1: rewards[1], 2: diffs[2][:, S:]}
-        last = keep.tile([P, S], F32, name="last")
         twos = {a: values[a][:, :S] for a in range(TILES)}
-        twos[2] = last[:]
         for a in (1, 0, 2, 3):
             nc.sync.dma_start(out=rewards[a], in_=rw_rows[a])
 
@@ -184,9 +182,10 @@ def tile_picked_gae8_none_p_kernel(tc, x_words, x_scales, w1, rw, offs, nx, out)
         b2 = fetch(diffs[1], DAMPING * DAMPING)
         fetch_add(d[3], values[3], rewards[3])
         nc.gpsimd.tensor_tensor(d[0][:, HALF:], less[0][:, HALF:], a1[:, HALF:], ADD)
-        c1 = fetch(values[2], DISCOUNT)
+        c1 = fetch(values[2], DISCOUNT, [(0, HALF), (HALF, SHARE)])
         reward_less_value(2, HALF, S)
         less_value(3, 0, S)
+        nc.vector.tensor_scalar(c1[:, SHARE:], following(values[2], SHARE, S), DISCOUNT, 0.0, MULT, ADD)
         d2 = fetch(diffs[3], DAMPING * DAMPING)
         damp_add(1, b2)
         add(d[2], less[2], c1[:])
@@ -202,11 +201,11 @@ def tile_picked_gae8_none_p_kernel(tc, x_words, x_scales, w1, rw, offs, nx, out)
         damp_add(2, c2)
         fetch_add(result[3][:], values[3], d[3], HALF, S)
         store(3, HALF, S)
-        c3 = fetch(last, 1.0, [(0, HALF), (HALF, SHARE)])
+        c3 = fetch(values[2], 1.0, [(0, HALF), (HALF, SHARE)])
         add(result[0][:], d[0], a3[:])
         store(0, 0, S)
         add(result[2][:, :HALF], d[2][:, :HALF], c3[:, :HALF])
         store(2, 0, HALF)
-        fetch_add(result[2][:], last, d[2], SHARE, S)
+        fetch_add(result[2][:], values[2], d[2], SHARE, S)
         add(result[2][:, HALF:SHARE], d[2][:, HALF:SHARE], c3[:, HALF:SHARE])
         store(2, HALF, S)

@@ -46,7 +46,7 @@ def tile_picked_gae8_none_p_kernel(tc, x_words, x_scales, w1, rw, offs, nx, out)
         all_words = keep.tile([P, T], U32, name="all_words", tag="words", align_bytes=64)
         all_scales = keep.tile([P, T], U8, name="all_scales", tag="scales", align_bytes=64)
         x_scale = keep.tile([P, S], U8, name="x_scale", align_bytes=64)
-        w_raw = [keep.tile([P, PACK // 2 * N], F32, name="w_raw%d" % h) for h in range(2)]
+        w_raw = keep.tile([P, 2, PACK // 2 * N], F32, name="w_raw", tag="w_raw")
 
         def row_tiles(name):
             return [keep.tile([P, S], F32, name="%s%d" % (name, a)) for a in range(TILES)]
@@ -54,19 +54,20 @@ def tile_picked_gae8_none_p_kernel(tc, x_words, x_scales, w1, rw, offs, nx, out)
         result = row_tiles("result")
         values = {0: keep.tile([P, 2 * S], F32, name="values0"), 2: keep.tile([P, S], F32, name="values2")}
         diffs = {a: keep.tile([P, 2 * S], F32, name="diffs%d" % a) for a in (2, 3)}
-        values[1], diffs[1] = w_raw
+        values[1] = keep.tile([P, 2 * S], F32, name="values1")
         ring = [keep.tile([P, S], F32, name="ring%d" % i) for i in range(RING)]
 
         nc.vector.memset(all_scales[:].bitcast(I32), 0)
         nc.vector.memset(x_scale[:].bitcast(I32), 0)
         for spare in (values[0], diffs[3]):
             nc.vector.memset(spare[:, S:], 0.0)
+        nc.scalar.copy(values[1][:, S:], values[0][:, S:])
 
         w_rows = w1.rearrange("(p h t) m -> h p (t m)", h=2, t=PACK // 2)
-        nc.sync.dma_start(out=w_raw[0][:], in_=w_rows[0])
+        nc.sync.dma_start(out=w_raw[:, 0], in_=w_rows[0])
         nc.sync.dma_start(picks[:], offs)
         nc.sync.dma_start(out=all_scales[:].bitcast(I32)[0:P:SPREAD, :], in_=x_scales[0].bitcast(I32))
-        nc.sync.dma_start(out=w_raw[1][:], in_=w_rows[1])
+        nc.sync.dma_start(out=w_raw[:, 1], in_=w_rows[1])
         nc.sync.dma_start(out=all_words[:].bitcast(I32), in_=x_words[0].rearrange("p c t -> p (c t)").bitcast(I32))
         nc.sync.dma_start(nexts[:], nx)
 
@@ -79,11 +80,11 @@ def tile_picked_gae8_none_p_kernel(tc, x_words, x_scales, w1, rw, offs, nx, out)
             )
 
         w_bf = keep.tile([P, TILES, P, PACK], BF16, name="w_bf", tag="w_bf", align_bytes=64)
-        src = [w_raw[h][:].rearrange("p (t c a) -> p c t a", t=PACK // 2, a=TILES) for h in range(2)]
-        dst = w_bf[:].rearrange("p a c (h t) -> p h c t a", h=2)
-        nc.scalar.copy(out=dst[:, 0], in_=src[0])
-        nc.vector.tensor_copy(out=dst[:, 1, :, :, 0:2], in_=src[1][:, :, :, 0:2])
-        nc.scalar.copy(out=dst[:, 1, :, :, 2:4], in_=src[1][:, :, :, 2:4])
+        src = w_raw[:].rearrange("p h (t c a) -> p c (h t) a", t=PACK // 2, a=TILES)
+        dst = w_bf[:].rearrange("p a c t -> p c t a")
+        nc.vector.tensor_copy(out=dst[:, :, :, 0:2], in_=src[:, :, :, 0:2])
+        nc.scalar.copy(out=dst[:, :, :, 2:4], in_=src[:, :, :, 2:4])
+        diffs[1] = keep.tile([P, 2 * S], F32, name="diffs1", tag="w_raw")
         w_code, w_scale = {}, {}
 
         def quantise(pair, tag):

@@ -104,10 +104,11 @@ def tile_picked_gae8_none_p_kernel(tc, x_words, x_scales, w1, rw, offs, nx, out)
             nc.vector.tensor_copy(x_code[:, lo:hi], all_words[:].indirect(picks[:, lo // GROUP : hi // GROUP]))
 
         values[3] = keep.tile([P, 2 * S], F32, name="values3", tag="scales", align_bytes=64)
-        diffs[0] = keep.tile([P, HALF + 2 * S], F32, name="diffs0", tag="w_bf", align_bytes=64)
+        diffs[0] = keep.tile([P, 3 * S], F32, name="diffs0", tag="w_bf", align_bytes=64)
         d = {a: diffs[a][:, :S] for a in range(TILES)}
-        rewards = {0: diffs[1][:, S:], 1: values[3][:, S:], 2: diffs[0][:, HALF + S :], 3: diffs[0][:, HALF : HALF + S]}
-        less = {0: rewards[0], 1: rewards[1], 2: diffs[2][:, S:]}
+        rewards = {0: diffs[1][:, S:], 1: values[3][:, S:], 2: diffs[0][:, 2 * S :], 3: diffs[0][:, S : 2 * S]}
+        less0 = keep.tile([P, S], F32, name="less0")
+        less = {0: less0[:], 1: rewards[1], 2: diffs[2][:, S:]}
         twos = {a: values[a][:, :S] for a in range(TILES)}
         for a in (1, 0, 2, 3):
             nc.sync.dma_start(out=rewards[a], in_=rw_rows[a])
@@ -125,13 +126,13 @@ def tile_picked_gae8_none_p_kernel(tc, x_words, x_scales, w1, rw, offs, nx, out)
             )
             return y
 
-        ys = {(a, lo): product(a, lo, hi) for a, (lo, hi) in zip((1, 0, 0, 1), (HALVES[0], HALVES[0], HALVES[1], HALVES[1]))}
-        ys[2, 0] = product(2, 0, HALF)
+        ys = {(a, lo): product(a, lo, hi) for a, (lo, hi) in zip((1, 0, 1, 0), (HALVES[0], HALVES[0], HALVES[1], HALVES[1]))}
         ys[3, 0] = product(3, 0, S)
+        ys[2, 0] = product(2, 0, HALF)
         ys[2, HALF] = product(2, HALF, S)
 
         def fill(a, lo, hi):
-            nc.scalar.activation(values[a][:, lo:hi], ys[a, lo][:], COPY, scale=DISCOUNT if a % 2 else 1.0)
+            nc.scalar.activation(values[a][:, lo:hi], ys[a, lo][:], COPY, scale=DISCOUNT if a else 1.0)
 
         def reward_less_value(a, lo, hi):
             nc.vector.tensor_tensor(less[a][:, lo:hi], rewards[a][:, lo:hi], ys[a, lo][:], SUBTRACT)
@@ -165,31 +166,30 @@ def tile_picked_gae8_none_p_kernel(tc, x_words, x_scales, w1, rw, offs, nx, out)
 
         fill(1, 0, HALF)
         fill(0, 0, HALF)
-        fill(0, HALF, S)
         fill(1, HALF, S)
+        fill(0, HALF, S)
+        fill(3, 0, S)
         reward_less_value(1, 0, HALF)
-        early = keep.tile([P, HALF], F32, name="early")
-        nc.gpsimd.tensor_tensor(early[:], rewards[0][:, :HALF], values[0][:, :HALF], SUBTRACT)
-        reward_less_value(0, HALF, S)
+        reward_less_value(0, 0, HALF)
+        fetch_add(d[1], values[1], rewards[1])
+        nc.gpsimd.tensor_tensor(less[0][:, HALF:], rewards[0][:, HALF:], values[0][:, HALF:S], SUBTRACT)
         a1 = result[0]
         nc.scalar.activation(a1[:], following(values[0], 0, S), COPY, scale=DISCOUNT)
-        fetch_add(d[1], values[1], rewards[1])
-        fill(3, 0, S)
         reward_less_value(2, 0, HALF)
-        nc.gpsimd.tensor_tensor(d[0][:, :HALF], early[:], a1[:, :HALF], ADD)
         fill(2, HALF, S)
         fill(2, 0, HALF)
         less_value(1, HALF, S)
         b2 = fetch(diffs[1], DAMPING * DAMPING)
         fetch_add(d[3], values[3], rewards[3])
-        nc.gpsimd.tensor_tensor(d[0][:, HALF:], less[0][:, HALF:], a1[:, HALF:], ADD)
-        c1 = fetch(values[2], DISCOUNT, [(0, HALF), (HALF, SHARE)])
+        nc.gpsimd.tensor_tensor(d[0][:, :SHARE], less[0][:, :SHARE], a1[:, :SHARE], ADD)
+        c1 = fetch(values[2], 1.0, HALVES[:1])
         reward_less_value(2, HALF, S)
         less_value(3, 0, S)
-        nc.vector.tensor_scalar(c1[:, SHARE:], following(values[2], SHARE, S), DISCOUNT, 0.0, MULT, ADD)
+        fetch_add(d[2], values[2], less[2], HALF, S)
+        add(d[0][:, SHARE:], less[0][:, SHARE:], a1[:, SHARE:])
         d2 = fetch(diffs[3], DAMPING * DAMPING)
         damp_add(1, b2)
-        add(d[2], less[2], c1[:])
+        add(d[2][:, :HALF], less[2][:, :HALF], c1[:, :HALF])
         a2 = fetch(diffs[0], DAMPING)
         fetch_add(result[1][:], values[1], d[1])
         store(1, 0, S)

@@ -127,7 +127,8 @@ def tile_picked_gae8_none_p_kernel(tc, x_words, x_scales, w1, rw, offs, nx, out)
             return y
 
         ys = {(a, lo): product(a, lo, hi) for a, (lo, hi) in zip((1, 0, 1, 0), (HALVES[0], HALVES[0], HALVES[1], HALVES[1]))}
-        ys[3, 0] = product(3, 0, S)
+        ys[3, 0] = product(3, 0, HALF)
+        ys[3, HALF] = product(3, HALF, S)
         ys[2, 0] = product(2, 0, HALF)
         ys[2, HALF] = product(2, HALF, S)
 
@@ -168,7 +169,8 @@ def tile_picked_gae8_none_p_kernel(tc, x_words, x_scales, w1, rw, offs, nx, out)
         fill(0, 0, HALF)
         fill(1, HALF, S)
         fill(0, HALF, S)
-        fill(3, 0, S)
+        fill(3, 0, HALF)
+        fill(3, HALF, S)
         reward_less_value(1, 0, HALF)
         reward_less_value(0, 0, HALF)
         fetch_add(d[1], values[1], rewards[1])
@@ -182,31 +184,35 @@ def tile_picked_gae8_none_p_kernel(tc, x_words, x_scales, w1, rw, offs, nx, out)
         b2 = fetch(diffs[1], DAMPING * DAMPING)
         fetch_add(d[3], values[3], rewards[3])
         nc.gpsimd.tensor_tensor(d[0][:, :SHARE], less[0][:, :SHARE], a1[:, :SHARE], ADD)
-        c1 = fetch(values[2], 1.0, HALVES[:1])
+        c1 = fetch(values[2], 1.0, [(0, HALF), (HALF, SHARE)])
         reward_less_value(2, HALF, S)
-        less_value(3, 0, S)
-        fetch_add(d[2], values[2], less[2], HALF, S)
+        less_value(3, 0, HALF)
+        less_value(3, HALF, S)
+        fetch_add(d[2], values[2], less[2], SHARE, S)
         add(d[0][:, SHARE:], less[0][:, SHARE:], a1[:, SHARE:])
         d2 = fetch(diffs[3], DAMPING * DAMPING)
         damp_add(1, b2)
-        add(d[2][:, :HALF], less[2][:, :HALF], c1[:, :HALF])
+        add(d[2][:, :SHARE], less[2][:, :SHARE], c1[:, :SHARE])
         a2 = fetch(diffs[0], DAMPING)
         fetch_add(result[1][:], values[1], d[1])
         store(1, 0, S)
         c2 = fetch(diffs[2], DAMPING * DAMPING)
         damp_add(3, d2)
         add(twos[0], d[0], a2[:])
-        a3 = fetch(values[0], DAMPING)
+        a3 = fetch(values[0], DAMPING, HALVES)
         fetch_add(result[3][:], values[3], d[3], 0, HALF)
         store(3, 0, HALF)
         damp_add(2, c2)
         fetch_add(result[3][:], values[3], d[3], HALF, S)
         store(3, HALF, S)
         c3 = fetch(values[2], 1.0, [(0, HALF), (HALF, SHARE)])
-        add(result[0][:], d[0], a3[:])
-        store(0, 0, S)
+        add(result[0][:, :HALF], d[0][:, :HALF], a3[:, :HALF])
+        store(0, 0, HALF)
+        fetch_add(result[2][:], values[2], d[2], SHARE, S)
+        store(2, SHARE, S)
+        add(result[0][:, HALF:], d[0][:, HALF:], a3[:, HALF:])
+        store(0, HALF, S)
         add(result[2][:, :HALF], d[2][:, :HALF], c3[:, :HALF])
         store(2, 0, HALF)
-        fetch_add(result[2][:], values[2], d[2], SHARE, S)
         add(result[2][:, HALF:SHARE], d[2][:, HALF:SHARE], c3[:, HALF:SHARE])
-        store(2, HALF, S)
+        store(2, HALF, SHARE)

from contextlib import ExitStack

import concourse.mybir as mybir

K, T, S, N = 512, 2048, 512, 512
FLOPS = 2 * K * N * S

F32 = mybir.dt.float32
BF16 = mybir.dt.bfloat16
I32 = mybir.dt.int32
U32 = mybir.dt.uint32
U16 = mybir.dt.uint16
U8 = mybir.dt.uint8
FP8X4 = mybir.dt.float8_e4m3fn_x4
ADD = mybir.AluOpType.add
MULT = mybir.AluOpType.mult
SUBTRACT = mybir.AluOpType.subtract
COPY = mybir.ActivationFunctionType.Copy

P = 128
PACK = 4
GROUP = 16
QUADRANT = 32
SCALE_ROWS = 4
SPREAD = 8
TILES = N // P
HALF = S // 2
HALVES = [(0, HALF), (HALF, S)]
DISCOUNT = 0.9
DAMPING = 0.75
SHARE = 384
RING = 3


def tile_picked_gae8_none_p_kernel(tc, x_words, x_scales, w1, rw, offs, nx, out):
    nc = tc.nc
    rw_rows = rw.rearrange("(p a) j -> a p j", a=TILES)
    out_rows = out.rearrange("(p a) j -> a p j", a=TILES)

    with ExitStack() as ctx:
        keep = ctx.enter_context(tc.tile_pool(name="keep", bufs=1))
        psum = ctx.enter_context(tc.psum_pool(name="psum", bufs=1))

        picks = keep.tile([P, S // GROUP], U16, name="picks")
        nexts = keep.tile([P, S // GROUP], U16, name="nexts")
        all_words = keep.tile([P, T], U32, name="all_words", tag="words", align_bytes=64)
        all_scales = keep.tile([P, T], U8, name="all_scales", tag="scales", align_bytes=64)
        x_scale = keep.tile([P, S], U8, name="x_scale", align_bytes=64)
        w_raw = keep.tile([P, 2, PACK // 2 * N], F32, name="w_raw", tag="w_raw")

        def row_tiles(name):
            return [keep.tile([P, S], F32, name="%s%d" % (name, a)) for a in range(TILES)]

        result = row_tiles("result")
        values = {0: keep.tile([P, 2 * S], F32, name="values0"), 2: keep.tile([P, S], F32, name="values2")}
        diffs = {a: keep.tile([P, 2 * S], F32, name="diffs%d" % a) for a in (2, 3)}
        values[1] = keep.tile([P, 2 * S], F32, name="values1")
        ring = [keep.tile([P, S], F32, name="ring%d" % i) for i in range(RING)]

        nc.vector.memset(all_scales[:].bitcast(I32), 0)
        nc.vector.memset(x_scale[:].bitcast(I32), 0)
        for spare in (values[0], diffs[3]):
            nc.vector.memset(spare[:, S:], 0.0)
        nc.scalar.copy(values[1][:, S:], values[0][:, S:])

        w_rows = w1.rearrange("(p h t) m -> h p (t m)", h=2, t=PACK // 2)
        nc.sync.dma_start(out=w_raw[:, 0], in_=w_rows[0])
        nc.sync.dma_start(picks[:], offs)
        nc.sync.dma_start(out=all_scales[:].bitcast(I32)[0:P:SPREAD, :], in_=x_scales[0].bitcast(I32))
        nc.sync.dma_start(out=w_raw[:, 1], in_=w_rows[1])
        nc.sync.dma_start(out=all_words[:].bitcast(I32), in_=x_words[0].rearrange("p c t -> p (c t)").bitcast(I32))
        nc.sync.dma_start(nexts[:], nx)

        picked_scales = keep.tile([P, S], U8, name="picked_scales", tag="picked", align_bytes=64)
        nc.vector.tensor_copy(picked_scales[:], all_scales[:].indirect(picks[:]))
        for r in range(SCALE_ROWS):
            nc.sync.dma_start(
                out=x_scale[:].bitcast(I32)[r:P:QUADRANT, :],
                in_=picked_scales[:].bitcast(I32)[r * SPREAD : P : QUADRANT, :],
            )

        w_bf = keep.tile([P, TILES, P, PACK], BF16, name="w_bf", tag="w_bf", align_bytes=64)
        src = w_raw[:].rearrange("p h (t c a) -> p c (h t) a", t=PACK // 2, a=TILES)
        dst = w_bf[:].rearrange("p a c t -> p c t a")
        nc.vector.tensor_copy(out=dst[:, :, :, 0:2], in_=src[:, :, :, 0:2])
        nc.scalar.copy(out=dst[:, :, :, 2:4], in_=src[:, :, :, 2:4])
        diffs[1] = keep.tile([P, 2 * S], F32, name="diffs1", tag="w_raw")
        w_code, w_scale = {}, {}

        def quantise(pair, tag):
            w_code[pair] = keep.tile([P, 2 * P], U32, name="w_code%d" % pair, tag=tag, align_bytes=64)
            w_scale[pair] = keep.tile([P, 2 * P], U8, name="w_scale%d" % pair, align_bytes=64)
            nc.vector.quantize_mx(
                out=w_code[pair][:].bitcast(FP8X4),
                scales=w_scale[pair][:],
                in_=w_bf[:, 2 * pair : 2 * pair + 2].rearrange("p a c t -> p (a c t)"),
            )

        quantise(0, "w_code0")
        quantise(1, "w_code1")

        x_code = keep.tile([P, S], U32, name="x_code", align_bytes=64)
        for lo, hi in HALVES:
            nc.vector.tensor_copy(x_code[:, lo:hi], all_words[:].indirect(picks[:, lo // GROUP : hi // GROUP]))

        values[3] = keep.tile([P, 2 * S], F32, name="values3", tag="scales", align_bytes=64)
        diffs[0] = keep.tile([P, 3 * S], F32, name="diffs0", tag="w_bf", align_bytes=64)
        d = {a: diffs[a][:, :S] for a in range(TILES)}
        rewards = {0: diffs[1][:, S:], 1: values[3][:, S:], 2: diffs[0][:, 2 * S :], 3: diffs[0][:, S : 2 * S]}
        less0 = keep.tile([P, S], F32, name="less0")
        less = {0: less0[:], 1: rewards[1], 2: diffs[2][:, S:]}
        twos = {a: values[a][:, :S] for a in range(TILES)}
        for a in (1, 0, 2, 3):
            nc.sync.dma_start(out=rewards[a], in_=rw_rows[a])

        def product(a, lo, hi):
            y = psum.tile([P, hi - lo], F32, name="y%d_%d" % (a, lo))
            nc.tensor.matmul_mx(
                out=y[:],
                lhsT=w_code[a // 2][:, a % 2 * P : (a % 2 + 1) * P].bitcast(FP8X4),
                lhsT_scale=w_scale[a // 2][:, a % 2 * P : (a % 2 + 1) * P],
                rhs=x_code[:, lo:hi].bitcast(FP8X4),
                rhs_scale=x_scale[:, lo:hi],
                start=True,
                stop=True,
            )
            return y

        ys = {(a, lo): product(a, lo, hi) for a, (lo, hi) in zip((1, 0, 1, 0), (HALVES[0], HALVES[0], HALVES[1], HALVES[1]))}
        ys[3, 0] = product(3, 0, HALF)
        ys[3, HALF] = product(3, HALF, S)
        ys[2, 0] = product(2, 0, HALF)
        ys[2, HALF] = product(2, HALF, S)

        def fill(a, lo, hi):
            nc.scalar.activation(values[a][:, lo:hi], ys[a, lo][:], COPY, scale=DISCOUNT if a else 1.0)

        def reward_less_value(a, lo, hi):
            nc.vector.tensor_tensor(less[a][:, lo:hi], rewards[a][:, lo:hi], ys[a, lo][:], SUBTRACT)

        def following(window, lo, hi):
            return window[:].indirect(nexts[:, lo // GROUP : hi // GROUP])

        fetched = []

        def fetch(window, scale, pieces=((0, S),)):
            slot = ring[len(fetched) % RING]
            fetched.append(slot)
            for lo, hi in pieces:
                nc.scalar.activation(slot[:, lo:hi], following(window, lo, hi), COPY, scale=scale)
            return slot

        def fetch_add(target, window, plain, lo=0, hi=S):
            nc.vector.tensor_tensor(target[:, lo:hi], following(window, lo, hi), plain[:, lo:hi], ADD)

        def store(a, lo, hi):
            nc.sync.dma_start(out=out_rows[a][:, lo:hi], in_=result[a][:, lo:hi])

        def add(target, one, other):
            nc.vector.tensor_tensor(target, one, other, ADD)

        def damp_add(a, got):
            nc.vector.scalar_tensor_tensor(twos[a], d[a], DAMPING, got[:], MULT, ADD)

        def less_value(a, lo, hi):
            nc.vector.tensor_tensor(d[a][:, lo:hi], d[a][:, lo:hi], ys[a, lo][:], SUBTRACT)

        fill(1, 0, HALF)
        fill(0, 0, HALF)
        fill(1, HALF, S)
        fill(0, HALF, S)
        fill(3, 0, HALF)
        fill(3, HALF, S)
        reward_less_value(1, 0, HALF)
        reward_less_value(0, 0, HALF)
        fetch_add(d[1], values[1], rewards[1])
        nc.gpsimd.tensor_tensor(less[0][:, HALF:], rewards[0][:, HALF:], values[0][:, HALF:S], SUBTRACT)
        a1 = result[0]
        nc.scalar.activation(a1[:], following(values[0], 0, S), COPY, scale=DISCOUNT)
        reward_less_value(2, 0, HALF)
        fill(2, HALF, S)
        fill(2, 0, HALF)
        less_value(1, HALF, S)
        b2 = fetch(diffs[1], DAMPING * DAMPING)
        fetch_add(d[3], values[3], rewards[3])
        nc.gpsimd.tensor_tensor(d[0][:, :SHARE], less[0][:, :SHARE], a1[:, :SHARE], ADD)
        c1 = fetch(values[2], 1.0, [(0, HALF), (HALF, SHARE)])
        reward_less_value(2, HALF, S)
        less_value(3, 0, HALF)
        less_value(3, HALF, S)
        fetch_add(d[2], values[2], less[2], SHARE, S)
        add(d[0][:, SHARE:], less[0][:, SHARE:], a1[:, SHARE:])
        d2 = fetch(diffs[3], DAMPING * DAMPING)
        damp_add(1, b2)
        add(d[2][:, :SHARE], less[2][:, :SHARE], c1[:, :SHARE])
        a2 = fetch(diffs[0], DAMPING)
        fetch_add(result[1][:], values[1], d[1])
        store(1, 0, S)
        c2 = fetch(diffs[2], DAMPING * DAMPING)
        damp_add(3, d2)
        add(twos[0], d[0], a2[:])
        a3 = fetch(values[0], DAMPING, HALVES)
        fetch_add(result[3][:], values[3], d[3], 0, HALF)
        store(3, 0, HALF)
        damp_add(2, c2)
        fetch_add(result[3][:], values[3], d[3], HALF, S)
        store(3, HALF, S)
        c3 = fetch(values[2], 1.0, [(0, HALF), (HALF, SHARE)])
        add(result[0][:, :HALF], d[0][:, :HALF], a3[:, :HALF])
        store(0, 0, HALF)
        fetch_add(result[2][:], values[2], d[2], SHARE, S)
        store(2, SHARE, S)
        add(result[0][:, HALF:], d[0][:, HALF:], a3[:, HALF:])
        store(0, HALF, S)
        add(result[2][:, :HALF], d[2][:, :HALF], c3[:, :HALF])
        store(2, 0, HALF)
        add(result[2][:, HALF:SHARE], d[2][:, HALF:SHARE], c3[:, HALF:SHARE])
        store(2, HALF, SHARE)
